import numpy as np, ml_dtypes
CORES = [3,7,11,15,131,135,139,143]
N = 8
BF = ml_dtypes.bfloat16
V, S, P, Q = 1, 2048, 16, 256
def fill(rng, l, cap):
    l = np.minimum(l, cap); e = S - int(np.sum(l)); o = rng.permutation(P); room = (cap - l)[o]; before = np.add.accumulate(room) - room
    l[o] += np.clip(e - before, 0, room); return l
def lens(rng, cap, g):
    c = np.sort(rng.permutation(S - 1)[:P - 1]) + 1
    return fill(rng, np.diff(np.concatenate([[0], c, [S]])), cap)
def put(d, v, g, a, l):
    j = v % V * P; d["frm"][v // V, g, j:j + P] = a; d["ln"][v // V, g, j:j + P] = l
def make(rng, lengths, share):
    d = {"frm": np.zeros((N, 8, V * P), np.int32), "ln": np.zeros((N, 8, V * P), np.int32), "lit": rng.integers(0, 256, (N, 8, Q)).astype(np.int32)}
    for v in range(N * V):
        for g in range(8):
            s = 1.0 if v == 0 else share[v, g]
            l = lengths(rng, Q if s == 1 else S, g); new = (rng.random(P) < s) & (l <= Q)
            put(d, v, g, np.where(new, S + rng.integers(0, np.maximum(Q - l, 0) + 1), rng.integers(0, S - l + 1)), l)
    return d
def setup_inputs(rng):
    return make(rng, lens, np.full((N * V, 8), 0.25))
def setup_inputs_long(rng):
    def lengths(rng, cap, g):
        l = fill(rng, np.ones(P, np.int64), cap)
        return np.sort(l)[::-1].copy() if g == 0 else np.sort(l) if g == 7 else l
    return make(rng, lengths, np.full((N * V, 8), 0.25))
def setup_inputs_ends(rng):
    d = make(rng, lambda rng, cap, g: np.full(P, S // P), np.full((N * V, 8), 0.25))
    k = rng.integers(0, 3, d["frm"].shape); new = d["frm"] >= S
    d["frm"] = np.where(k == 0, np.where(new, S, 0), np.where(k == 1, np.where(new, S + Q, S) - d["ln"], d["frm"])).astype(np.int32)
    return d
def setup_inputs_moves(rng):
    d = setup_inputs(rng)
    for v in range(1, N * V):
        for g in range(8):
            l = lens(rng, S, g); c = np.add.accumulate(l) - l; p = np.arange(P) if g == v % 8 else rng.permutation(P)
            put(d, v, g, c[p], l[p])
    return d
def setup_inputs_spread(rng):
    share = rng.choice(np.array([0, 0.125, 0.5, 1]), (N * V, 8)); share[N * V - 1, 0] = 0; share[N * V - 1, 1] = 1
    d = make(rng, lambda rng, cap, g: fill(rng, 1 + rng.multinomial(S - P, rng.dirichlet(np.full(P, 0.125))), cap), share)
    d["lit"] = np.where(rng.random(d["lit"].shape) < 0.5, 255 * rng.integers(0, 2, d["lit"].shape), d["lit"]).astype(np.int32)
    return d
def check_inputs(d):
    bad = []; a = np.asarray(d["frm"]).astype(np.int64).reshape(N, 8, V, P); l = np.asarray(d["ln"]).astype(np.int64).reshape(N, 8, V, P); t = np.asarray(d["lit"])
    if (l < 1).any() or (np.sum(l, axis=3) != S).any(): bad.append("lengths")
    copied = (a >= 0) & (a + l <= S); new = (a >= S) & (a + l <= S + Q)
    if not (copied | new).all(): bad.append("pieces")
    if not new[0, :, 0].all(): bad.append("version 0")
    if (t < 0).any() or (t > 255).any(): bad.append("literals")
    return bad
def reference(frm, ln, lit):
    y = np.zeros((N, 8, V * S), np.float32); old = np.zeros((8, S), np.int64)
    for v in range(N * V):
        r, k = v // V, v % V; src = np.concatenate([old, lit[r]], axis=1); new = np.zeros((8, S), np.int64)
        for g in range(8):
            a = frm[r, g, k * P:(k + 1) * P]; l = ln[r, g, k * P:(k + 1) * P]; first = np.add.accumulate(l) - l
            new[g] = src[g][np.repeat(a - first, l) + np.arange(S)]
        y[r, :, k * S:(k + 1) * S] = new; old = new
    return {"y": y}

@@ -1,0 +1,245 @@
+from concourse.bass import DstId, RemoteDMATransfer
+from concourse.mybir import dt, AluOpType, AxisListType, ActivationFunctionType
+
+N = 8
+BASE = 1792
+BIG = 1.5 * 2.0 ** 35
+BATCH = (6, 5, 3, 2)
+LO = [0, 0, 0, 0, 0, 0, 1, 2]
+
+SCRATCH = {
+    "fi": ("sbuf", [128, 16], "int32"),
+    "li": ("sbuf", [128, 16], "int32"),
+    "lt": ("sbuf", [128, 256], "int32"),
+    "lb": ("sbuf", [128, 256], "bfloat16"),
+    "ki": ("sbuf", [128, 128], "int32"),
+    "ke": ("sbuf", [128, 128], "int32"),
+    "kx": ("sbuf", [128, 128], "int32"),
+    "kp": ("sbuf", [128, 8], "int32"),
+    "km": ("sbuf", [128, 8], "int32"),
+    "kf": ("sbuf", [128, 8], "float32"),
+    "ident": ("sbuf", [128, 128], "float16"),
+    "ee": ("sbuf", [128, 128], "float16"),
+    "lcode": ("sbuf", [128, 16], "int32"),
+    "gs": ("sbuf", [128, 16], "int32"),
+    "lnf": ("sbuf", [128, 32], "float32"),
+    "hs": ("sbuf", [128, 32], "float32"),
+    "ff": ("sbuf", [128, 16], "float32"),
+    "dd": ("sbuf", [128, 16], "float32"),
+    "dr": ("sbuf", [128, 16], "float32"),
+    "ta": ("sbuf", [128, 32], "float16"),
+    "tabs": ("sbuf", [128, 256], "float32"),
+    "xa": ("sbuf", [128, 128], "float16"),
+    "xb": ("sbuf", [128, 128], "float16"),
+    "tt": ("sbuf", [128, 2048], "float16"),
+    "rr": ("sbuf", [128, 128], "float32"),
+    "offs": ("sbuf", [128, 128], "uint16"),
+    "lst": ("sbuf", [128, 128], "uint16"),
+    "land0": ("sbuf", [128, 128], "uint16"),
+    "land1": ("sbuf", [128, 128], "uint16"),
+    "zb": ("sbuf", [128, 256], "bfloat16"),
+    "lz": ("sbuf", [128, 256], "bfloat16"),
+    "wa": ("sbuf", [128, 2304], "bfloat16"),
+    "wb": ("sbuf", [128, 3840], "bfloat16"),
+    "yo": ("sbuf", [128, 2048], "float32"),
+    "litd": ("dram", [8, 128, 16], "bfloat16"),
+    "pt": ("psum", [128, 512], "float32"),
+    "ps": ("psum", [128, 512], "float32"),
+}
+SEMAPHORES = (["gi", "zz", "vm", "kc", "ks", "sx", "di", "dl", "dlit", "vp", "pp", "vt", "cv", "st", "sr", "so", "sl", "pe",
+               "sz", "fw", "dw", "dz", "da", "sg", "sa", "dy", "ls"]
+              + ["tb%d" % b for b in range(len(BATCH))] + ["tab%d" % v for v in range(N)] + ["lit%d" % v for v in range(N)]
+              + ["list0", "list1"])
+
+
+def rank_program(g, core, T, topo):
+    r = T.rank_of(core)
+    if r is None:
+        return
+    A = AluOpType
+    COPY = ActivationFunctionType.Copy
+    sem = T.sem
+    V, S, PE, Y = g.vector, g.scalar, g.tensor, g.sync
+    lo = LO[r]
+    steps = list(range(r, lo - 1, -1))
+
+    def shared_engines(src, dsts):
+        es = topo.engines(src, dsts[0])
+        for d in dsts[1:]:
+            es = [e for e in es if e in topo.engines(src, d)]
+        return es[:8]
+
+    sent = [0]
+
+    def send(ranks, src, dst, sname):
+        cores = [T.cores[q] for q in ranks]
+        es = shared_engines(core, cores)
+        mask = 0
+        for e in es:
+            mask |= 1 << e
+        ids = []
+        for c in cores:
+            rid, pid = topo.addr(c, core)
+            ids.append(DstId(rid=rid, pnc=pid))
+        g.remote_dma_fused([RemoteDMATransfer(dst_ids=ids, dma_engine_mask=mask, remote_sem=sem[sname], srcs=[src],
+                                              dsts=[dst] * len(ids), alu_op=0)], local_sem=sem.ls)
+        sent[0] += len(es)
+
+    def got(q):
+        return len(shared_engines(T.cores[q[0]], [T.cores[d] for d in q[1]]))
+
+    tab_to = [[q for q in range(v + 1, N) if LO[q] <= v] for v in range(N)]
+    list_to = [[q for q in range(N) if LO[q] > v] for v in range(2)]
+    fast = list_to[0]
+    lit_to = [[q for q in range(v + 1, N) if not (v == 0 and q in fast)] for v in range(N)]
+
+    S.dma_start(T.fi[0:8, :], T.frm[:, :]).then_inc(sem.di, 16)
+    Y.dma_start(T.li[0:8, :], T.ln[:, :]).then_inc(sem.dl, 16)
+    if r == 0:
+        lt, lb = T.lt[:, 0:16], T.lb[:, 0:16]
+    else:
+        lt, lb = T.lt[0:8, :], T.lb[0:8, :]
+    Y.dma_start(lt, T.lit[:, :]).then_inc(sem.dlit, 16)
+
+    g.iota(T.ki[:], [[1, 128]], 0, -1).then_inc(sem.gi, 1)
+    g.iota(T.ke[0:8, :], [[1, 8], [0, 16]], 0, -1).then_inc(sem.gi, 1)
+    g.iota(T.kp[:, 0:1], [[1, 1]], 0, 1).then_inc(sem.gi, 1)
+    g.iota(T.kx[:], [[16, 128]], 0, 0).then_inc(sem.gi, 1)
+
+    V.memset(T.zb[:], 0.0).then_inc(sem.zz, 1)
+    V.memset(T.lnf[0:8, 0:1], 0.0).then_inc(sem.vm, 1)
+    V.memset(T.hs[0:8, 0:1], 0.0).then_inc(sem.vm, 1)
+    V.wait_ge(sem.gi, 4)
+    V.tensor_scalar(T.km[:, 0:1], T.kp[:, 0:1], 15, None, A.bitwise_and).then_inc(sem.ks, 1)
+    V.tensor_scalar(T.ee[0:8, :], T.ke[0:8, :], 0, None, A.is_equal).then_inc(sem.kc, 1)
+    V.wait_ge(sem.ks, 1)
+    V.tensor_copy(T.kf[:, 0:1], T.km[:, 0:1]).then_inc(sem.ks, 1)
+    V.tensor_scalar(T.ident[:], T.ki[:], 0, None, A.is_equal).then_inc(sem.kc, 1)
+    V.wait_ge(sem.ks, 2)
+    V.tensor_scalar(T.xa[:], T.kx[:], T.kf[:, 0:1], None, A.add).then_inc(sem.sx, 1)
+
+    V.wait_ge(sem.vm, 2)
+    V.wait_ge(sem.di, 16)
+    V.tensor_scalar(T.lcode[0:8, :], T.fi[0:8, :], 2048, -(2048 + 256 * r), A.is_ge, A.mult).then_inc(sem.vp, 1)
+    V.wait_ge(sem.dl, 16)
+    V.tensor_tensor(T.gs[0:8, :], T.fi[0:8, :], T.li[0:8, :], A.add).then_inc(sem.vp, 1)
+    V.tensor_copy(T.lnf[0:8, 1:17], T.li[0:8, :]).then_inc(sem.vp, 1)
+    V.wait_ge(sem.vp, 3)
+    V.tensor_tensor(T.ff[0:8, :], T.fi[0:8, :], T.lcode[0:8, :], A.add).then_inc(sem.vp, 1)
+    V.tensor_tensor(T.hs[0:8, 1:17], T.gs[0:8, :], T.lcode[0:8, :], A.add).then_inc(sem.vp, 1)
+    V.tensor_tensor_scan(T.ta[0:8, 0:16], T.lnf[0:8, 0:16], T.lnf[0:8, 0:16], 0.0, A.add, A.max).then_inc(sem.vp, 1)
+    V.wait_ge(sem.vp, 6)
+    V.tensor_tensor(T.dd[0:8, :], T.ff[0:8, :], T.hs[0:8, 0:16], A.subtract).then_inc(sem.vp, 1)
+    V.wait_ge(sem.vp, 7)
+    V.tensor_scalar(T.dr[0:8, :], T.dd[0:8, :], BIG, BIG, A.add, A.subtract).then_inc(sem.vp, 1)
+    V.wait_ge(sem.vp, 8)
+    V.tensor_tensor(T.ta[0:8, 16:32], T.dd[0:8, :], T.dr[0:8, :], A.subtract).then_inc(sem.vp, 1)
+    if r == 0:
+        V.wait_ge(sem.dlit, 16)
+        V.tensor_copy(lb, lt).then_inc(sem.cv, 1)
+    PE.wait_ge(sem.kc, 2)
+    PE.wait_ge(sem.vp, 9)
+    PE.matmul(T.pt[:, 0:32], T.ee[0:8, :], T.ta[0:8, :], True, True).then_inc(sem.pp, 1)
+    V.wait_ge(sem.pp, 1)
+    V.tensor_copy(T.tabs[:, 32 * r:32 * r + 32], T.pt[:, 0:32]).then_inc(sem.vt, 1)
+    if r > 0:
+        V.wait_ge(sem.dlit, 16)
+        V.tensor_copy(lb, lt).then_inc(sem.cv, 1)
+
+    V.wait_ge(sem.vt, 1)
+    xs = [T.xa, T.xb]
+    for s, v in enumerate(steps):
+        xi, xo = xs[s % 2], xs[(s + 1) % 2]
+        if s > 0:
+            V.wait_ge(sem["tab%d" % v], got((v, tab_to[v])))
+        V.wait_ge(sem.sx, s + 1)
+        PE.wait_ge(sem.sx, s + 1)
+        PE.matmul(T.ps[:, 0:128], T.ident[:], xi[:], True, False).then_inc(sem.pe, 1)
+        j = 0
+        for b, n in enumerate(BATCH):
+            tb = sem["tb%d" % b]
+            for k in range(j, j + n):
+                c = 32 * v + k
+                V.tensor_scalar(T.tt[:, 128 * k:128 * k + 128], xi[:], T.tabs[:, c:c + 1], T.tabs[:, c + 16:c + 17],
+                                A.is_ge, A.mult).then_inc(tb, 1)
+            PE.wait_ge(tb, n * (s + 1))
+            for k in range(j, j + n):
+                PE.matmul(T.ps[:, 0:128], T.ident[:], T.tt[:, 128 * k:128 * k + 128], False, k == 15).then_inc(sem.pe, 1)
+            j += n
+        V.wait_ge(sem.pe, 17 * (s + 1))
+        V.tensor_scalar(T.rr[:], T.ps[:, 0:128], BIG, BIG, A.add, A.subtract).then_inc(sem.sr, 1)
+        V.wait_ge(sem.sr, s + 1)
+        V.tensor_tensor(xo[:], T.ps[:, 0:128], T.rr[:], A.subtract).then_inc(sem.sx, 1)
+        if r == 1 and s == 0:
+            V.wait_ge(sem.sx, 2)
+            V.tensor_scalar(T.lst[:], xo[:], 256, None, A.add).then_inc(sem.sl, 1)
+    V.wait_ge(sem.sx, len(steps) + 1)
+    V.tensor_scalar(T.offs[:], xs[len(steps) % 2][:], 256 * r, None, A.add).then_inc(sem.so, 1)
+
+    if r == 0:
+        g.wait_ge(sem.cv, 1)
+        send(fast, lb, T.litd[0], "lit0")
+    if tab_to[r]:
+        g.wait_ge(sem.vt, 1)
+        send(tab_to[r], T.tabs[:, 32 * r:32 * r + 32], T.tabs[:, 32 * r:32 * r + 32], "tab%d" % r)
+    if r == 0:
+        g.wait_ge(sem.so, 1)
+        send(list_to[0], T.offs[:], T.land0[:], "list0")
+    if r == 1:
+        g.wait_ge(sem.sl, 1)
+        send(list_to[1], T.lst[:], T.land1[:], "list1")
+    if lit_to[r]:
+        g.wait_ge(sem.st, 16)
+        send(lit_to[r], T.litd[r], T.litd[r], "lit%d" % r)
+    if sent[0]:
+        g.wait_ge(sem.ls, sent[0])
+
+    zeros = [T.wb[:, 256 * (7 - v):256 * (8 - v)] for v in range(r, (0 if lo == 0 else 1) - 1, -1)]
+    if lo > 0:
+        zeros.append(T.lz[:])
+    if lo > 1:
+        zeros.append(T.wa[:, 0:256])
+    S.wait_ge(sem.zz, 1)
+    for z in zeros[::-1]:
+        S.activation(z, T.zb[:], COPY).then_inc(sem.sz, 1)
+
+    Y.wait_ge(sem.cv, 1)
+    Y.dma_start(T.litd[r], lb).then_inc(sem.st, 16)
+    Y.wait_ge(sem.sz, len(zeros))
+    nw = 0
+    for v in [r] + list(range(r)):
+        if v == r:
+            Y.wait_ge(sem.st, 16)
+        else:
+            Y.wait_ge(sem["lit%d" % v], got((v, fast if (v == 0 and r in fast) else lit_to[v])))
+        if v >= lo:
+            Y.dma_start(T.wb[0:128:16, 256 * (7 - v):256 * (8 - v)], T.litd[v]).then_inc(sem.dw, 16)
+            nw += 1
+        elif v == 0:
+            Y.dma_start(T.lz[0:128:16, :], T.litd[v]).then_inc(sem.dz, 16)
+        else:
+            Y.dma_start(T.wa[0:128:16, 0:256], T.litd[v]).then_inc(sem.da, 16)
+
+    for k in range(lo):
+        win = T.lz[:] if k == 0 else T.wa[:]
+        out = T.wb[:, BASE:BASE + 2048] if k == lo - 1 else T.wa[:, 256:2304]
+        S.wait_ge(sem["list%d" % k], got((k, list_to[k])))
+        S.wait_ge(sem.dz if k == 0 else sem.da, 16)
+        if k > 0:
+            S.wait_ge(sem.fw, k)
+        S.activation(out, win.indirect(T["land%d" % k][:, 0:128]), COPY).then_inc(sem.fw, 1)
+
+    end = BASE + (2048 if lo > 0 else 256)
+    win = T.wb[:, 256 * (7 - r):end]
+    for q in (V, S):
+        q.wait_ge(sem.dw, 16 * nw)
+        if lo > 0:
+            q.wait_ge(sem.fw, lo)
+        q.wait_ge(sem.so, 1)
+    V.tensor_copy(T.yo[:, 0:1024], win.indirect(T.offs[:, 0:64])).then_inc(sem.sg, 1)
+    S.activation(T.yo[:, 1024:2048], win.indirect(T.offs[:, 64:128]), COPY).then_inc(sem.sa, 1)
+    Y.wait_ge(sem.sg, 1)
+    Y.dma_start(T.y[:, 0:1024], T.yo[0:128:16, 0:1024]).then_inc(sem.dy, 16)
+    S.wait_ge(sem.sa, 1)
+    S.dma_start(T.y[:, 1024:2048], T.yo[0:128:16, 1024:2048]).then_inc(sem.dy, 16)
+    Y.wait_ge(sem.dy, 32)

@@ -5,7 +5,8 @@ N = 8
 BASE = 1792
 BIG = 1.5 * 2.0 ** 35
 BATCH = (6, 5, 3, 2)
-LO = [0, 0, 0, 0, 0, 0, 1, 2]
+LO = [0, 0, 0, 0, 0, 1, 2, 3]
+FWD = max(LO)
 
 SCRATCH = {
     "fi": ("sbuf", [128, 16], "int32"),
@@ -35,21 +36,22 @@ SCRATCH = {
     "rr": ("sbuf", [128, 128], "float32"),
     "offs": ("sbuf", [128, 128], "uint16"),
     "lst": ("sbuf", [128, 128], "uint16"),
-    "land0": ("sbuf", [128, 128], "uint16"),
-    "land1": ("sbuf", [128, 128], "uint16"),
     "zb": ("sbuf", [128, 256], "bfloat16"),
-    "lz": ("sbuf", [128, 256], "bfloat16"),
-    "wa": ("sbuf", [128, 2304], "bfloat16"),
+    "wa0": ("sbuf", [128, 256], "bfloat16"),
     "wb": ("sbuf", [128, 3840], "bfloat16"),
     "yo": ("sbuf", [128, 2048], "float32"),
     "litd": ("dram", [8, 128, 16], "bfloat16"),
     "pt": ("psum", [128, 512], "float32"),
     "ps": ("psum", [128, 512], "float32"),
 }
+for _k in range(FWD):
+    SCRATCH["land%d" % _k] = ("sbuf", [128, 128], "uint16")
+    if _k > 0:
+        SCRATCH["wa%d" % _k] = ("sbuf", [128, 256 * _k + 2048], "bfloat16")
 SEMAPHORES = (["gi", "zz", "vm", "kc", "ks", "sx", "di", "dl", "dlit", "vp", "pp", "vt", "cv", "st", "sr", "so", "sl", "pe",
-               "sz", "fw", "dw", "dz", "da", "sg", "sa", "dy", "ls"]
+               "sz", "fw", "dw", "sg", "sa", "dy", "ls"]
               + ["tb%d" % b for b in range(len(BATCH))] + ["tab%d" % v for v in range(N)] + ["lit%d" % v for v in range(N)]
-              + ["list0", "list1"])
+              + ["list%d" % k for k in range(FWD)] + ["dz%d" % k for k in range(FWD)])
 
 
 def rank_program(g, core, T, topo):
@@ -89,7 +91,7 @@ def rank_program(g, core, T, topo):
         return len(shared_engines(T.cores[q[0]], [T.cores[d] for d in q[1]]))
 
     tab_to = [[q for q in range(v + 1, N) if LO[q] <= v] for v in range(N)]
-    list_to = [[q for q in range(N) if LO[q] > v] for v in range(2)]
+    list_to = [[q for q in range(N) if LO[q] > v] for v in range(FWD)]
     fast = list_to[0]
     lit_to = [[q for q in range(v + 1, N) if not (v == 0 and q in fast)] for v in range(N)]
 
@@ -170,9 +172,9 @@ def rank_program(g, core, T, topo):
         V.tensor_scalar(T.rr[:], T.ps[:, 0:128], BIG, BIG, A.add, A.subtract).then_inc(sem.sr, 1)
         V.wait_ge(sem.sr, s + 1)
         V.tensor_tensor(xo[:], T.ps[:, 0:128], T.rr[:], A.subtract).then_inc(sem.sx, 1)
-        if r == 1 and s == 0:
+        if 0 < r < FWD and s == 0:
             V.wait_ge(sem.sx, 2)
-            V.tensor_scalar(T.lst[:], xo[:], 256, None, A.add).then_inc(sem.sl, 1)
+            V.tensor_scalar(T.lst[:], xo[:], 256 * r, None, A.add).then_inc(sem.sl, 1)
     V.wait_ge(sem.sx, len(steps) + 1)
     V.tensor_scalar(T.offs[:], xs[len(steps) % 2][:], 256 * r, None, A.add).then_inc(sem.so, 1)
 
@@ -182,25 +184,22 @@ def rank_program(g, core, T, topo):
     if tab_to[r]:
         g.wait_ge(sem.vt, 1)
         send(tab_to[r], T.tabs[:, 32 * r:32 * r + 32], T.tabs[:, 32 * r:32 * r + 32], "tab%d" % r)
-    if r == 0:
-        g.wait_ge(sem.so, 1)
-        send(list_to[0], T.offs[:], T.land0[:], "list0")
-    if r == 1:
-        g.wait_ge(sem.sl, 1)
-        send(list_to[1], T.lst[:], T.land1[:], "list1")
+    if r < FWD:
+        src, ready = (T.offs, sem.so) if r == 0 else (T.lst, sem.sl)
+        g.wait_ge(ready, 1)
+        send(list_to[r], src[:], T["land%d" % r][:], "list%d" % r)
     if lit_to[r]:
         g.wait_ge(sem.st, 16)
         send(lit_to[r], T.litd[r], T.litd[r], "lit%d" % r)
     if sent[0]:
         g.wait_ge(sem.ls, sent[0])
 
-    zeros = [T.wb[:, 256 * (7 - v):256 * (8 - v)] for v in range(r, (0 if lo == 0 else 1) - 1, -1)]
-    if lo > 0:
-        zeros.append(T.lz[:])
-    if lo > 1:
-        zeros.append(T.wa[:, 0:256])
+    zeros = []
+    for k in range(lo):
+        zeros += [T["wa%d" % k][:, 256 * i:256 * i + 256] for i in range(max(k, 1))]
+    zeros += [T.wb[:, 256 * (7 - v):256 * (8 - v)] for v in range(0 if lo == 0 else 1, r + 1)]
     S.wait_ge(sem.zz, 1)
-    for z in zeros[::-1]:
+    for z in zeros:
         S.activation(z, T.zb[:], COPY).then_inc(sem.sz, 1)
 
     Y.wait_ge(sem.cv, 1)
@@ -215,19 +214,17 @@ def rank_program(g, core, T, topo):
         if v >= lo:
             Y.dma_start(T.wb[0:128:16, 256 * (7 - v):256 * (8 - v)], T.litd[v]).then_inc(sem.dw, 16)
             nw += 1
-        elif v == 0:
-            Y.dma_start(T.lz[0:128:16, :], T.litd[v]).then_inc(sem.dz, 16)
         else:
-            Y.dma_start(T.wa[0:128:16, 0:256], T.litd[v]).then_inc(sem.da, 16)
+            Y.dma_start(T["wa%d" % v][0:128:16, 0:256], T.litd[v]).then_inc(sem["dz%d" % v], 16)
 
     for k in range(lo):
-        win = T.lz[:] if k == 0 else T.wa[:]
-        out = T.wb[:, BASE:BASE + 2048] if k == lo - 1 else T.wa[:, 256:2304]
+        nxt = T.wb if k == lo - 1 else T["wa%d" % (k + 1)]
+        at = BASE if k == lo - 1 else 256 * (k + 1)
         S.wait_ge(sem["list%d" % k], got((k, list_to[k])))
-        S.wait_ge(sem.dz if k == 0 else sem.da, 16)
+        S.wait_ge(sem["dz%d" % k], 16)
         if k > 0:
             S.wait_ge(sem.fw, k)
-        S.activation(out, win.indirect(T["land%d" % k][:, 0:128]), COPY).then_inc(sem.fw, 1)
+        S.activation(nxt[:, at:at + 2048], T["wa%d" % k][:].indirect(T["land%d" % k][:, 0:128]), COPY).then_inc(sem.fw, 1)
 
     end = BASE + (2048 if lo > 0 else 256)
     win = T.wb[:, 256 * (7 - r):end]

@@ -4,7 +4,7 @@ from concourse.mybir import dt, AluOpType, AxisListType, ActivationFunctionType
 N = 8
 BASE = 1792
 BIG = 1.5 * 2.0 ** 35
-BATCH = (6, 5, 3, 2)
+BATCH = (6, 4, 3, 2, 1)
 LO = [0, 0, 0, 0, 0, 1, 2, 3]
 FWD = max(LO)
 
@@ -21,14 +21,9 @@ SCRATCH = {
     "kf": ("sbuf", [128, 8], "float32"),
     "ident": ("sbuf", [128, 128], "float16"),
     "ee": ("sbuf", [128, 128], "float16"),
-    "lcode": ("sbuf", [128, 16], "int32"),
-    "gs": ("sbuf", [128, 16], "int32"),
-    "lnf": ("sbuf", [128, 32], "float32"),
-    "hs": ("sbuf", [128, 32], "float32"),
-    "ff": ("sbuf", [128, 16], "float32"),
-    "dd": ("sbuf", [128, 16], "float32"),
+    "en": ("sbuf", [128, 128], "float16"),
+    "cb": ("sbuf", [128, 128], "float16"),
     "dr": ("sbuf", [128, 16], "float32"),
-    "ta": ("sbuf", [128, 32], "float16"),
     "tabs": ("sbuf", [128, 256], "float32"),
     "xa": ("sbuf", [128, 128], "float16"),
     "xb": ("sbuf", [128, 128], "float16"),
@@ -48,7 +43,7 @@ for _k in range(FWD):
     SCRATCH["land%d" % _k] = ("sbuf", [128, 128], "uint16")
     if _k > 0:
         SCRATCH["wa%d" % _k] = ("sbuf", [128, 256 * _k + 2048], "bfloat16")
-SEMAPHORES = (["gi", "zz", "vm", "kc", "ks", "sx", "di", "dl", "dlit", "vp", "pp", "vt", "cv", "st", "sr", "so", "sl", "pe",
+SEMAPHORES = (["gi", "zz", "kc", "ks", "sx", "di", "dl", "dlit", "vp", "vr", "pp", "vt", "cv", "st", "sr", "so", "sl", "pe",
                "sz", "fw", "dw", "sg", "sa", "dy", "ls"]
               + ["tb%d" % b for b in range(len(BATCH))] + ["tab%d" % v for v in range(N)] + ["lit%d" % v for v in range(N)]
               + ["list%d" % k for k in range(FWD)] + ["dz%d" % k for k in range(FWD)])
@@ -109,46 +104,48 @@ def rank_program(g, core, T, topo):
     g.iota(T.kx[:], [[16, 128]], 0, 0).then_inc(sem.gi, 1)
 
     V.memset(T.zb[:], 0.0).then_inc(sem.zz, 1)
-    V.memset(T.lnf[0:8, 0:1], 0.0).then_inc(sem.vm, 1)
-    V.memset(T.hs[0:8, 0:1], 0.0).then_inc(sem.vm, 1)
     V.wait_ge(sem.gi, 4)
     V.tensor_scalar(T.km[:, 0:1], T.kp[:, 0:1], 15, None, A.bitwise_and).then_inc(sem.ks, 1)
+    V.tensor_scalar(T.cb[0:8, :], T.ki[0:8, :], 0, None, A.mult).then_inc(sem.kc, 1)
     V.tensor_scalar(T.ee[0:8, :], T.ke[0:8, :], 0, None, A.is_equal).then_inc(sem.kc, 1)
+    V.tensor_scalar(T.en[0:8, :], T.ke[0:8, :], 0, -1, A.is_equal, A.mult).then_inc(sem.kc, 1)
     V.wait_ge(sem.ks, 1)
     V.tensor_copy(T.kf[:, 0:1], T.km[:, 0:1]).then_inc(sem.ks, 1)
     V.tensor_scalar(T.ident[:], T.ki[:], 0, None, A.is_equal).then_inc(sem.kc, 1)
     V.wait_ge(sem.ks, 2)
     V.tensor_scalar(T.xa[:], T.kx[:], T.kf[:, 0:1], None, A.add).then_inc(sem.sx, 1)
 
-    V.wait_ge(sem.vm, 2)
+    c1, c2, cl, cn = 0, 17, 34, 51
+    V.wait_ge(sem.kc, 4)
     V.wait_ge(sem.di, 16)
-    V.tensor_scalar(T.lcode[0:8, :], T.fi[0:8, :], 2048, -(2048 + 256 * r), A.is_ge, A.mult).then_inc(sem.vp, 1)
+    V.tensor_scalar(T.cb[0:8, c1 + 1:c1 + 17], T.fi[0:8, :], 2047, None, A.min).then_inc(sem.vp, 1)
+    V.tensor_scalar(T.cb[0:8, c2 + 1:c2 + 17], T.fi[0:8, :], 2047, 2047, A.max, A.subtract).then_inc(sem.vp, 1)
+    V.tensor_scalar(T.cb[0:8, cl + 1:cl + 17], T.fi[0:8, :], 2048, -(2048 + 256 * r), A.is_ge, A.mult).then_inc(sem.vp, 1)
     V.wait_ge(sem.dl, 16)
-    V.tensor_tensor(T.gs[0:8, :], T.fi[0:8, :], T.li[0:8, :], A.add).then_inc(sem.vp, 1)
-    V.tensor_copy(T.lnf[0:8, 1:17], T.li[0:8, :]).then_inc(sem.vp, 1)
-    V.wait_ge(sem.vp, 3)
-    V.tensor_tensor(T.ff[0:8, :], T.fi[0:8, :], T.lcode[0:8, :], A.add).then_inc(sem.vp, 1)
-    V.tensor_tensor(T.hs[0:8, 1:17], T.gs[0:8, :], T.lcode[0:8, :], A.add).then_inc(sem.vp, 1)
-    V.tensor_tensor_scan(T.ta[0:8, 0:16], T.lnf[0:8, 0:16], T.lnf[0:8, 0:16], 0.0, A.add, A.max).then_inc(sem.vp, 1)
-    V.wait_ge(sem.vp, 6)
-    V.tensor_tensor(T.dd[0:8, :], T.ff[0:8, :], T.hs[0:8, 0:16], A.subtract).then_inc(sem.vp, 1)
-    V.wait_ge(sem.vp, 7)
-    V.tensor_scalar(T.dr[0:8, :], T.dd[0:8, :], BIG, BIG, A.add, A.subtract).then_inc(sem.vp, 1)
-    V.wait_ge(sem.vp, 8)
-    V.tensor_tensor(T.ta[0:8, 16:32], T.dd[0:8, :], T.dr[0:8, :], A.subtract).then_inc(sem.vp, 1)
+    V.tensor_copy(T.cb[0:8, cn + 1:cn + 17], T.li[0:8, :]).then_inc(sem.vp, 1)
+    PE.wait_ge(sem.kc, 4)
+    PE.wait_ge(sem.vp, 4)
+    parts = [(T.ee, c1 + 1), (T.en, c1), (T.ee, c2 + 1), (T.en, c2), (T.ee, cl + 1), (T.en, cl), (T.en, cn)]
+    for i, (w, c) in enumerate(parts):
+        PE.matmul(T.pt[:, 16:32], w[0:8, :], T.cb[0:8, c:c + 16], i == 0, i == len(parts) - 1).then_inc(sem.pp, 1)
+    PE.matmul(T.pt[:, 0:16], T.ee[0:8, :], T.cb[0:8, cn:cn + 16], True, True).then_inc(sem.pp, 1)
     if r == 0:
         V.wait_ge(sem.dlit, 16)
         V.tensor_copy(lb, lt).then_inc(sem.cv, 1)
-    PE.wait_ge(sem.kc, 2)
-    PE.wait_ge(sem.vp, 9)
-    PE.matmul(T.pt[:, 0:32], T.ee[0:8, :], T.ta[0:8, :], True, True).then_inc(sem.pp, 1)
-    V.wait_ge(sem.pp, 1)
-    V.tensor_copy(T.tabs[:, 32 * r:32 * r + 32], T.pt[:, 0:32]).then_inc(sem.vt, 1)
+    V.wait_ge(sem.pp, len(parts) + 1)
+    tc = 32 * r
     if r > 0:
+        V.tensor_scalar(T.dr[:], T.pt[:, 16:32], BIG, BIG, A.add, A.subtract).then_inc(sem.vr, 1)
+    V.tensor_tensor_scan(T.tabs[:, tc:tc + 16], T.pt[:, 0:16], T.zb[:, 0:16], 0.0, A.add, A.add).then_inc(sem.vt, 1)
+    if r > 0:
+        V.wait_ge(sem.vr, 1)
+        V.tensor_tensor(T.tabs[:, tc + 16:tc + 32], T.pt[:, 16:32], T.dr[:], A.subtract).then_inc(sem.vt, 1)
         V.wait_ge(sem.dlit, 16)
         V.tensor_copy(lb, lt).then_inc(sem.cv, 1)
+    else:
+        V.tensor_copy(T.tabs[:, tc + 16:tc + 32], T.pt[:, 16:32]).then_inc(sem.vt, 1)
 
-    V.wait_ge(sem.vt, 1)
+    V.wait_ge(sem.vt, 2)
     xs = [T.xa, T.xb]
     for s, v in enumerate(steps):
         xi, xo = xs[s % 2], xs[(s + 1) % 2]
@@ -169,21 +166,26 @@ def rank_program(g, core, T, topo):
                 PE.matmul(T.ps[:, 0:128], T.ident[:], T.tt[:, 128 * k:128 * k + 128], False, k == 15).then_inc(sem.pe, 1)
             j += n
         V.wait_ge(sem.pe, 17 * (s + 1))
+        if r == 0:
+            break
         V.tensor_scalar(T.rr[:], T.ps[:, 0:128], BIG, BIG, A.add, A.subtract).then_inc(sem.sr, 1)
         V.wait_ge(sem.sr, s + 1)
         V.tensor_tensor(xo[:], T.ps[:, 0:128], T.rr[:], A.subtract).then_inc(sem.sx, 1)
-        if 0 < r < FWD and s == 0:
+        if r < FWD and s == 0:
             V.wait_ge(sem.sx, 2)
             V.tensor_scalar(T.lst[:], xo[:], 256 * r, None, A.add).then_inc(sem.sl, 1)
-    V.wait_ge(sem.sx, len(steps) + 1)
-    V.tensor_scalar(T.offs[:], xs[len(steps) % 2][:], 256 * r, None, A.add).then_inc(sem.so, 1)
+    if r == 0:
+        V.tensor_copy(T.offs[:], T.ps[:, 0:128]).then_inc(sem.so, 1)
+    else:
+        V.wait_ge(sem.sx, len(steps) + 1)
+        V.tensor_scalar(T.offs[:], xs[len(steps) % 2][:], 256 * r, None, A.add).then_inc(sem.so, 1)
 
     if r == 0:
         g.wait_ge(sem.cv, 1)
         send(fast, lb, T.litd[0], "lit0")
     if tab_to[r]:
-        g.wait_ge(sem.vt, 1)
-        send(tab_to[r], T.tabs[:, 32 * r:32 * r + 32], T.tabs[:, 32 * r:32 * r + 32], "tab%d" % r)
+        g.wait_ge(sem.vt, 2)
+        send(tab_to[r], T.tabs[:, tc:tc + 32], T.tabs[:, tc:tc + 32], "tab%d" % r)
     if r < FWD:
         src, ready = (T.offs, sem.so) if r == 0 else (T.lst, sem.sl)
         g.wait_ge(ready, 1)
@@ -201,6 +203,7 @@ def rank_program(g, core, T, topo):
     S.wait_ge(sem.zz, 1)
     for z in zeros:
         S.activation(z, T.zb[:], COPY).then_inc(sem.sz, 1)
+    V.wait_ge(sem.zz, 1)
 
     Y.wait_ge(sem.cv, 1)
     Y.dma_start(T.litd[r], lb).then_inc(sem.st, 16)

@@ -2,51 +2,89 @@ from concourse.bass import DstId, RemoteDMATransfer
 from concourse.mybir import dt, AluOpType, AxisListType, ActivationFunctionType
 
 N = 8
-BASE = 1792
+PAD = 32
 BIG = 1.5 * 2.0 ** 35
-BATCH = (6, 4, 3, 2, 1)
-LO = [0, 0, 0, 0, 0, 1, 2, 3]
-FWD = max(LO)
+B16 = 1.5 * 2.0 ** 27
+B8 = 1.5 * 2.0 ** 26
+SIZE = [1, 1, 1, 2, 1, 2, 1, 2]
+
+
+def below(r):
+    out, b = [], r - SIZE[r]
+    while b >= 0:
+        out.append(b)
+        b -= SIZE[b]
+    return out[::-1]
+
+
+USED = sorted({b for r in range(N) for b in below(r)})
+DEPTH = max(len(below(r)) for r in range(N)) + 1
 
 SCRATCH = {
-    "fi": ("sbuf", [128, 16], "int32"),
-    "li": ("sbuf", [128, 16], "int32"),
-    "lt": ("sbuf", [128, 256], "int32"),
-    "lb": ("sbuf", [128, 256], "bfloat16"),
-    "ki": ("sbuf", [128, 128], "int32"),
-    "ke": ("sbuf", [128, 128], "int32"),
-    "kx": ("sbuf", [128, 128], "int32"),
-    "kp": ("sbuf", [128, 8], "int32"),
-    "km": ("sbuf", [128, 8], "int32"),
-    "kf": ("sbuf", [128, 8], "float32"),
+    "fi": ("sbuf", [128, 1], "int32"),
+    "li": ("sbuf", [128, 1], "int32"),
+    "lt": ("sbuf", [128, 16], "int32"),
+    "lb": ("sbuf", [128, 16], "bfloat16"),
+    "kp": ("sbuf", [128, 1], "int32"),
+    "ka": ("sbuf", [128, 1], "int32"),
+    "ki": ("sbuf", [128, 128], "bfloat16"),
+    "kq": ("sbuf", [128, 128], "bfloat16"),
+    "mq": ("sbuf", [128, 128], "bfloat16"),
+    "kc": ("sbuf", [128, 128], "bfloat16"),
+    "nf": ("sbuf", [128, 1], "float32"),
+    "pf": ("sbuf", [128, 1], "float32"),
+    "mf": ("sbuf", [128, 1], "float32"),
+    "cs": ("sbuf", [128, 1], "float16"),
+    "ch": ("sbuf", [128, 1], "float16"),
+    "cg": ("sbuf", [128, 1], "float16"),
+    "tri": ("sbuf", [128, 128], "float16"),
     "ident": ("sbuf", [128, 128], "float16"),
-    "ee": ("sbuf", [128, 128], "float16"),
-    "en": ("sbuf", [128, 128], "float16"),
-    "cb": ("sbuf", [128, 128], "float16"),
-    "dr": ("sbuf", [128, 16], "float32"),
-    "tabs": ("sbuf", [128, 256], "float32"),
+    "nsh": ("sbuf", [128, 128], "float16"),
+    "dif": ("sbuf", [128, 128], "float16"),
+    "mask": ("sbuf", [128, 128], "float16"),
+    "mqm": ("sbuf", [128, 128], "float16"),
+    "oh": ("sbuf", [128, 16], "float16"),
     "xa": ("sbuf", [128, 128], "float16"),
-    "xb": ("sbuf", [128, 128], "float16"),
+    "f1": ("sbuf", [128, 1], "float16"),
+    "f2": ("sbuf", [128, 1], "float16"),
+    "ln16": ("sbuf", [128, 1], "float16"),
+    "hi": ("sbuf", [128, 1], "float32"),
+    "lo": ("sbuf", [128, 1], "float32"),
+    "r16": ("sbuf", [128, 1], "float32"),
+    "fr": ("sbuf", [128, 1], "float32"),
+    "rd": ("sbuf", [128, 1], "float32"),
+    "dm": ("sbuf", [128, 1], "float32"),
+    "tsb": ("sbuf", [128, 32], "float16"),
+    "tabs": ("sbuf", [128, 32], "float32"),
+    "tland": ("sbuf", [128, 32], "float32"),
+    "v1h": ("sbuf", [128, 128], "float16"),
+    "v2h": ("sbuf", [128, 128], "float16"),
+    "v1l": ("sbuf", [128, 128], "float16"),
+    "v2l": ("sbuf", [128, 128], "float16"),
+    "bst": ("sbuf", [128, 128], "float16"),
+    "xf": ("sbuf", [128, 128], "float16"),
     "tt": ("sbuf", [128, 2048], "float16"),
     "rr": ("sbuf", [128, 128], "float32"),
+    "xo": ("sbuf", [128, 128], "float16"),
     "offs": ("sbuf", [128, 128], "uint16"),
-    "lst": ("sbuf", [128, 128], "uint16"),
-    "zb": ("sbuf", [128, 256], "bfloat16"),
-    "wa0": ("sbuf", [128, 256], "bfloat16"),
-    "wb": ("sbuf", [128, 3840], "bfloat16"),
+    "zb": ("sbuf", [128, PAD + 512], "bfloat16"),
     "yo": ("sbuf", [128, 2048], "float32"),
     "litd": ("dram", [8, 128, 16], "bfloat16"),
+    "pa": ("psum", [128, 512], "float32"),
+    "pb": ("psum", [128, 512], "float32"),
+    "pd": ("psum", [128, 512], "float32"),
     "pt": ("psum", [128, 512], "float32"),
-    "ps": ("psum", [128, 512], "float32"),
+    "p0": ("psum", [128, 512], "float32"),
+    "p1": ("psum", [128, 512], "float32"),
 }
-for _k in range(FWD):
-    SCRATCH["land%d" % _k] = ("sbuf", [128, 128], "uint16")
-    if _k > 0:
-        SCRATCH["wa%d" % _k] = ("sbuf", [128, 256 * _k + 2048], "bfloat16")
-SEMAPHORES = (["gi", "zz", "kc", "ks", "sx", "di", "dl", "dlit", "vp", "vr", "pp", "vt", "cv", "st", "sr", "so", "sl", "pe",
-               "sz", "fw", "dw", "sg", "sa", "dy", "ls"]
-              + ["tb%d" % b for b in range(len(BATCH))] + ["tab%d" % v for v in range(N)] + ["lit%d" % v for v in range(N)]
-              + ["list%d" % k for k in range(FWD)] + ["dz%d" % k for k in range(FWD)])
+for _b in USED:
+    SCRATCH["land%d" % _b] = ("sbuf", [128, 128], "uint16")
+for _k in range(DEPTH):
+    SCRATCH["w%d" % _k] = ("sbuf", [128, PAD + 256 if _k == 0 else PAD + 512 + 2048], "bfloat16")
+SEMAPHORES = (["di", "dl", "dlit", "st", "dy", "ls", "tabw"]
+              + ["a%d" % i for i in range(80)]
+              + ["sz%d" % k for k in range(DEPTH)] + ["dw%d" % k for k in range(DEPTH)]
+              + ["lit%d" % v for v in range(N)] + ["list%d" % b for b in USED])
 
 
 def rank_program(g, core, T, topo):
@@ -57,8 +95,9 @@ def rank_program(g, core, T, topo):
     COPY = ActivationFunctionType.Copy
     sem = T.sem
     V, S, PE, Y = g.vector, g.scalar, g.tensor, g.sync
-    lo = LO[r]
-    steps = list(range(r, lo - 1, -1))
+    n = SIZE[r]
+    fwd = below(r)
+    chain = fwd + [r]
 
     def shared_engines(src, dsts):
         es = topo.engines(src, dsts[0])
@@ -82,164 +121,218 @@ def rank_program(g, core, T, topo):
                                               dsts=[dst] * len(ids), alu_op=0)], local_sem=sem.ls)
         sent[0] += len(es)
 
-    def got(q):
-        return len(shared_engines(T.cores[q[0]], [T.cores[d] for d in q[1]]))
+    def got(v, ranks):
+        return len(shared_engines(T.cores[v], [T.cores[d] for d in ranks]))
 
-    tab_to = [[q for q in range(v + 1, N) if LO[q] <= v] for v in range(N)]
-    list_to = [[q for q in range(N) if LO[q] > v] for v in range(FWD)]
-    fast = list_to[0]
-    lit_to = [[q for q in range(v + 1, N) if not (v == 0 and q in fast)] for v in range(N)]
+    down = range(N - 1, -1, -1)
+    list_to = {b: [q for q in down if b in below(q)] for b in range(N)}
+    tab_to = {v: [q for q in range(N) if SIZE[q] == 2 and q == v + 1] for v in range(N)}
+    fast = [q for q in down if len(below(q)) == DEPTH - 1]
+    lit_to = {v: [q for q in down if q > v and not (v == 0 and q in fast)] for v in range(N)}
 
-    S.dma_start(T.fi[0:8, :], T.frm[:, :]).then_inc(sem.di, 16)
-    Y.dma_start(T.li[0:8, :], T.ln[:, :]).then_inc(sem.dl, 16)
-    if r == 0:
-        lt, lb = T.lt[:, 0:16], T.lb[:, 0:16]
-    else:
-        lt, lb = T.lt[0:8, :], T.lb[0:8, :]
-    Y.dma_start(lt, T.lit[:, :]).then_inc(sem.dlit, 16)
+    count = [0]
+    seen = set()
 
-    g.iota(T.ki[:], [[1, 128]], 0, -1).then_inc(sem.gi, 1)
-    g.iota(T.ke[0:8, :], [[1, 8], [0, 16]], 0, -1).then_inc(sem.gi, 1)
-    g.iota(T.kp[:, 0:1], [[1, 1]], 0, 1).then_inc(sem.gi, 1)
-    g.iota(T.kx[:], [[16, 128]], 0, 0).then_inc(sem.gi, 1)
+    def new():
+        count[0] += 1
+        return "a%d" % (count[0] - 1)
 
-    V.memset(T.zb[:], 0.0).then_inc(sem.zz, 1)
-    V.wait_ge(sem.gi, 4)
-    V.tensor_scalar(T.km[:, 0:1], T.kp[:, 0:1], 15, None, A.bitwise_and).then_inc(sem.ks, 1)
-    V.tensor_scalar(T.cb[0:8, :], T.ki[0:8, :], 0, None, A.mult).then_inc(sem.kc, 1)
-    V.tensor_scalar(T.ee[0:8, :], T.ke[0:8, :], 0, None, A.is_equal).then_inc(sem.kc, 1)
-    V.tensor_scalar(T.en[0:8, :], T.ke[0:8, :], 0, -1, A.is_equal, A.mult).then_inc(sem.kc, 1)
-    V.wait_ge(sem.ks, 1)
-    V.tensor_copy(T.kf[:, 0:1], T.km[:, 0:1]).then_inc(sem.ks, 1)
-    V.tensor_scalar(T.ident[:], T.ki[:], 0, None, A.is_equal).then_inc(sem.kc, 1)
-    V.wait_ge(sem.ks, 2)
-    V.tensor_scalar(T.xa[:], T.kx[:], T.kf[:, 0:1], None, A.add).then_inc(sem.sx, 1)
+    def vop(ins):
+        s = new()
+        ins.then_inc(sem[s], 1)
+        return s
 
-    c1, c2, cl, cn = 0, 17, 34, 51
-    V.wait_ge(sem.kc, 4)
-    V.wait_ge(sem.di, 16)
-    V.tensor_scalar(T.cb[0:8, c1 + 1:c1 + 17], T.fi[0:8, :], 2047, None, A.min).then_inc(sem.vp, 1)
-    V.tensor_scalar(T.cb[0:8, c2 + 1:c2 + 17], T.fi[0:8, :], 2047, 2047, A.max, A.subtract).then_inc(sem.vp, 1)
-    V.tensor_scalar(T.cb[0:8, cl + 1:cl + 17], T.fi[0:8, :], 2048, -(2048 + 256 * r), A.is_ge, A.mult).then_inc(sem.vp, 1)
-    V.wait_ge(sem.dl, 16)
-    V.tensor_copy(T.cb[0:8, cn + 1:cn + 17], T.li[0:8, :]).then_inc(sem.vp, 1)
-    PE.wait_ge(sem.kc, 4)
-    PE.wait_ge(sem.vp, 4)
-    parts = [(T.ee, c1 + 1), (T.en, c1), (T.ee, c2 + 1), (T.en, c2), (T.ee, cl + 1), (T.en, cl), (T.en, cn)]
-    for i, (w, c) in enumerate(parts):
-        PE.matmul(T.pt[:, 16:32], w[0:8, :], T.cb[0:8, c:c + 16], i == 0, i == len(parts) - 1).then_inc(sem.pp, 1)
-    PE.matmul(T.pt[:, 0:16], T.ee[0:8, :], T.cb[0:8, cn:cn + 16], True, True).then_inc(sem.pp, 1)
-    if r == 0:
-        V.wait_ge(sem.dlit, 16)
-        V.tensor_copy(lb, lt).then_inc(sem.cv, 1)
-    V.wait_ge(sem.pp, len(parts) + 1)
-    tc = 32 * r
-    if r > 0:
-        V.tensor_scalar(T.dr[:], T.pt[:, 16:32], BIG, BIG, A.add, A.subtract).then_inc(sem.vr, 1)
-    V.tensor_tensor_scan(T.tabs[:, tc:tc + 16], T.pt[:, 0:16], T.zb[:, 0:16], 0.0, A.add, A.add).then_inc(sem.vt, 1)
-    if r > 0:
-        V.wait_ge(sem.vr, 1)
-        V.tensor_tensor(T.tabs[:, tc + 16:tc + 32], T.pt[:, 16:32], T.dr[:], A.subtract).then_inc(sem.vt, 1)
-        V.wait_ge(sem.dlit, 16)
-        V.tensor_copy(lb, lt).then_inc(sem.cv, 1)
-    else:
-        V.tensor_copy(T.tabs[:, tc + 16:tc + 32], T.pt[:, 16:32]).then_inc(sem.vt, 1)
+    def need(q, name, *ss):
+        for s in ss:
+            s, k = s if isinstance(s, tuple) else (s, 1)
+            if (name, s) not in seen:
+                seen.add((name, s))
+                q.wait_ge(sem[s], k)
 
-    V.wait_ge(sem.vt, 2)
-    xs = [T.xa, T.xb]
-    for s, v in enumerate(steps):
-        xi, xo = xs[s % 2], xs[(s + 1) % 2]
-        if s > 0:
-            V.wait_ge(sem["tab%d" % v], got((v, tab_to[v])))
-        V.wait_ge(sem.sx, s + 1)
-        PE.wait_ge(sem.sx, s + 1)
-        PE.matmul(T.ps[:, 0:128], T.ident[:], xi[:], True, False).then_inc(sem.pe, 1)
-        j = 0
-        for b, n in enumerate(BATCH):
-            tb = sem["tb%d" % b]
-            for k in range(j, j + n):
-                c = 32 * v + k
-                V.tensor_scalar(T.tt[:, 128 * k:128 * k + 128], xi[:], T.tabs[:, c:c + 1], T.tabs[:, c + 16:c + 17],
-                                A.is_ge, A.mult).then_inc(tb, 1)
-            PE.wait_ge(tb, n * (s + 1))
-            for k in range(j, j + n):
-                PE.matmul(T.ps[:, 0:128], T.ident[:], T.tt[:, 128 * k:128 * k + 128], False, k == 15).then_inc(sem.pe, 1)
-            j += n
-        V.wait_ge(sem.pe, 17 * (s + 1))
-        if r == 0:
-            break
-        V.tensor_scalar(T.rr[:], T.ps[:, 0:128], BIG, BIG, A.add, A.subtract).then_inc(sem.sr, 1)
-        V.wait_ge(sem.sr, s + 1)
-        V.tensor_tensor(xo[:], T.ps[:, 0:128], T.rr[:], A.subtract).then_inc(sem.sx, 1)
-        if r < FWD and s == 0:
-            V.wait_ge(sem.sx, 2)
-            V.tensor_scalar(T.lst[:], xo[:], 256 * r, None, A.add).then_inc(sem.sl, 1)
-    if r == 0:
-        V.tensor_copy(T.offs[:], T.ps[:, 0:128]).then_inc(sem.so, 1)
-    else:
-        V.wait_ge(sem.sx, len(steps) + 1)
-        V.tensor_scalar(T.offs[:], xs[len(steps) % 2][:], 256 * r, None, A.add).then_inc(sem.so, 1)
+    def vneed(*ss):
+        need(V, "v", *ss)
 
-    if r == 0:
-        g.wait_ge(sem.cv, 1)
-        send(fast, lb, T.litd[0], "lit0")
+    def pneed(*ss):
+        need(PE, "p", *ss)
+
+    S.dma_start(T.fi[:, 0:1], T.frm[:, :]).then_inc(sem.di, 16)
+    Y.dma_start(T.li[:, 0:1], T.ln[:, :]).then_inc(sem.dl, 16)
+    S.dma_start(T.lt[:, :], T.lit[:, :]).then_inc(sem.dlit, 16)
+
+    g0 = vop(g.iota(T.kp[:, 0:1], [[1, 1]], 0, 1))
+    g1 = vop(g.iota(T.ki[:], [[1, 128]], 0, -1, allow_small_or_imprecise_dtypes=True))
+    g2 = vop(g.iota(T.kq[:], [[16, 8], [0, 16]], 0, 0, allow_small_or_imprecise_dtypes=True))
+    g3 = vop(g.iota(T.mq[:], [[0, 8], [1, 16]], 1, 0, allow_small_or_imprecise_dtypes=True))
+    g4 = vop(g.iota(T.kc[:], [[16, 128]], 0, 0, allow_small_or_imprecise_dtypes=True))
+
+    zz = vop(V.memset(T.zb[:], 0.0))
+    vneed(g0)
+    ka = vop(V.tensor_scalar(T.ka[:], T.kp[:], 15, None, A.bitwise_and))
+    vneed(g1)
+    tri = vop(V.tensor_scalar(T.tri[:], T.ki[:], 0, None, A.is_gt))
+    ident = vop(V.tensor_scalar(T.ident[:], T.ki[:], 0, None, A.is_equal))
+    vneed(ka)
+    nf = vop(V.tensor_scalar(T.nf[:], T.ka[:], 15, -1, A.is_lt, A.mult))
+    pf = vop(V.tensor_tensor(T.pf[:], T.kp[:], T.ka[:], A.subtract))
+    cs = vop(V.tensor_scalar(T.cs[:], T.ka[:], 0, -256 * n, A.mult, A.add))
+    ch = vop(V.tensor_scalar(T.ch[:], T.ka[:], 0, -7.5, A.mult, A.add))
+    mf = vop(V.tensor_copy(T.mf[:], T.ka[:]))
+    vneed(nf)
+    nsh = vop(V.tensor_scalar(T.nsh[:], T.ki[:], 1, T.nf[:, 0:1], A.is_equal, A.mult))
+    vneed(pf)
+    cg = vop(V.tensor_scalar(T.cg[:], T.pf[:], -128, None, A.mult))
+    vneed(ident, nsh)
+    dif = vop(V.tensor_tensor(T.dif[:], T.ident[:], T.nsh[:], A.add))
+    vneed(g2)
+    mask = vop(V.tensor_scalar(T.mask[:], T.kq[:], T.pf[:, 0:1], None, A.is_equal))
+    vneed(g3, mask)
+    mqm = vop(V.tensor_tensor(T.mqm[:], T.mq[:], T.mask[:], A.mult))
+    vneed(mf)
     if tab_to[r]:
-        g.wait_ge(sem.vt, 2)
-        send(tab_to[r], T.tabs[:, tc:tc + 32], T.tabs[:, tc:tc + 32], "tab%d" % r)
-    if r < FWD:
-        src, ready = (T.offs, sem.so) if r == 0 else (T.lst, sem.sl)
-        g.wait_ge(ready, 1)
-        send(list_to[r], src[:], T["land%d" % r][:], "list%d" % r)
+        oh = vop(V.tensor_scalar(T.oh[:], T.mq[:, 0:16], 1, T.mf[:, 0:1], A.subtract, A.is_equal))
+
+    sd, sa, sb = new(), new(), new()
+    pneed(dif, cs, ident, cg, ch)
+    PE.matmul(T.pd[:, 0:1], T.dif[:], T.cs[:], True, False).then_inc(sem[sd], 1)
+    PE.matmul(T.pb[:, 0:1], T.ident[:], T.cg[:], True, False).then_inc(sem[sb], 1)
+    PE.matmul(T.pb[:, 0:1], T.ident[:], T.ch[:], False, False).then_inc(sem[sb], 1)
+    PE.matmul(T.pa[:, 0:1], T.ident[:], T.cg[:], True, False).then_inc(sem[sa], 1)
+
+    V.wait_ge(sem.di, 16)
+    f1 = vop(V.tensor_scalar(T.f1[:], T.fi[:], 2048, None, A.subtract))
+    f2 = vop(V.tensor_scalar(T.f2[:], T.fi[:], 2048, 2048 + 256 * n, A.is_lt, A.mult))
+    V.wait_ge(sem.dl, 16)
+    l16 = vop(V.tensor_copy(T.ln16[:], T.li[:]))
+    pneed(f1, f2)
+    PE.matmul(T.pd[:, 0:1], T.dif[:], T.f1[:], False, False).then_inc(sem[sd], 1)
+    PE.matmul(T.pd[:, 0:1], T.dif[:], T.f2[:], False, False).then_inc(sem[sd], 1)
+    pneed(l16, nsh, tri)
+    PE.matmul(T.pd[:, 0:1], T.nsh[:], T.ln16[:], False, True).then_inc(sem[sd], 1)
+    PE.matmul(T.pb[:, 0:1], T.tri[:], T.ln16[:], False, True).then_inc(sem[sb], 1)
+    PE.matmul(T.pa[:, 0:1], T.tri[:], T.ln16[:], False, True).then_inc(sem[sa], 1)
+    vneed(g4)
+    xa = vop(V.tensor_scalar(T.xa[:], T.kc[:], T.mf[:, 0:1], None, A.add))
+    V.wait_ge(sem.dlit, 16)
+    cv = vop(V.tensor_copy(T.lb[:], T.lt[:]))
+    sd, sa, sb = (sd, 4), (sa, 2), (sb, 3)
+    s0 = new()
+    pneed(xa)
+    PE.matmul(T.p0[:, 0:128], T.ident[:], T.xa[:], True, False).then_inc(sem[s0], 1)
+
+    vneed(sd)
+    if tab_to[r]:
+        rd = vop(V.tensor_scalar(T.rd[:], T.pd[:, 0:1], BIG, BIG, A.add, A.subtract))
+    hi = vop(V.tensor_scalar(T.hi[:], T.pd[:, 0:1], B8, B8, A.add, A.subtract))
+    vneed(sb)
+    r16 = vop(V.tensor_scalar(T.r16[:], T.pb[:, 0:1], B16, B16, A.add, A.subtract))
+    vneed(sa)
+    if tab_to[r]:
+        vneed(rd)
+        dm = vop(V.tensor_tensor(T.dm[:], T.pd[:, 0:1], T.rd[:], A.subtract))
+        vneed(oh)
+        t1 = vop(V.tensor_scalar(T.tsb[:, 0:16], T.oh[:], T.pa[:, 0:1], None, A.mult))
+        vneed(dm)
+        t2 = vop(V.tensor_scalar(T.tsb[:, 16:32], T.oh[:], T.dm[:, 0:1], None, A.mult))
+        pneed(mask, t1, t2)
+        pt = vop(PE.matmul(T.pt[:, 0:32], T.mask[:], T.tsb[:], True, True))
+    vneed(hi)
+    lo = vop(V.tensor_tensor(T.lo[:], T.pd[:, 0:1], T.hi[:], A.subtract))
+    vneed(r16)
+    fr = vop(V.tensor_tensor(T.fr[:], T.pa[:, 0:1], T.r16[:], A.subtract))
+    v1h = vop(V.tensor_scalar(T.v1h[:], T.kc[:], T.r16[:, 0:1], T.hi[:, 0:1], A.is_gt, A.mult))
+    if tab_to[r]:
+        vneed(pt)
+        tabs = vop(V.tensor_copy(T.tabs[:], T.pt[:, 0:32]))
+    v2h = vop(V.tensor_scalar(T.v2h[:], T.kc[:], T.r16[:, 0:1], T.hi[:, 0:1], A.is_equal, A.mult))
+    vneed(lo)
+    v1l = vop(V.tensor_scalar(T.v1l[:], T.kc[:], T.r16[:, 0:1], T.lo[:, 0:1], A.is_gt, A.mult))
+    vneed(fr, mqm)
+    bst = vop(V.tensor_scalar(T.bst[:], T.mqm[:], T.fr[:, 0:1], None, A.is_gt))
+    v2l = vop(V.tensor_scalar(T.v2l[:], T.kc[:], T.r16[:, 0:1], T.lo[:, 0:1], A.is_equal, A.mult))
+    pneed(mask, v1h)
+    PE.matmul(T.p0[:, 0:128], T.mask[:], T.v1h[:], False, False).then_inc(sem[s0], 1)
+    pneed(v1l)
+    PE.matmul(T.p0[:, 0:128], T.mask[:], T.v1l[:], False, False).then_inc(sem[s0], 1)
+    pneed(bst, v2h)
+    PE.matmul(T.p0[:, 0:128], T.bst[:], T.v2h[:], False, False).then_inc(sem[s0], 1)
+    pneed(v2l)
+    PE.matmul(T.p0[:, 0:128], T.bst[:], T.v2l[:], False, True).then_inc(sem[s0], 1)
+    vneed((s0, 5))
+    if n == 1:
+        offs = vop(V.tensor_scalar(T.offs[:], T.p0[:, 0:128], 256 * n + PAD, None, A.add))
+    else:
+        xf = vop(V.tensor_copy(T.xf[:], T.p0[:, 0:128]))
+        s1 = new()
+        vneed(xf)
+        V.wait_ge(sem.tabw, got(r - 1, tab_to[r - 1]))
+        pneed(xf)
+        PE.matmul(T.p1[:, 0:128], T.ident[:], T.xf[:], True, False).then_inc(sem[s1], 1)
+        for k in range(16):
+            t = vop(V.tensor_scalar(T.tt[:, 128 * k:128 * k + 128], T.xf[:], T.tland[:, k:k + 1], T.tland[:, k + 16:k + 17],
+                                    A.is_ge, A.mult))
+            pneed(t)
+            PE.matmul(T.p1[:, 0:128], T.ident[:], T.tt[:, 128 * k:128 * k + 128], False, k == 15).then_inc(sem[s1], 1)
+        vneed((s1, 17))
+        rr = vop(V.tensor_scalar(T.rr[:], T.p1[:, 0:128], BIG, BIG, A.add, A.subtract))
+        vneed(rr)
+        xo = vop(V.tensor_tensor(T.xo[:], T.p1[:, 0:128], T.rr[:], A.subtract))
+        vneed(xo)
+        offs = vop(V.tensor_scalar(T.offs[:], T.xo[:], 256 * n + PAD, None, A.add))
+
+    if r == 0:
+        need(g, "g", cv)
+        send(fast, T.lb[:], T.litd[0], "lit0")
+    if tab_to[r]:
+        need(g, "g", tabs)
+        send(tab_to[r], T.tabs[:], T.tland[:], "tabw")
     if lit_to[r]:
         g.wait_ge(sem.st, 16)
         send(lit_to[r], T.litd[r], T.litd[r], "lit%d" % r)
+    if list_to[r]:
+        need(g, "g", offs)
+        send(list_to[r], T.offs[:], T["land%d" % r][:], "list%d" % r)
     if sent[0]:
         g.wait_ge(sem.ls, sent[0])
 
-    zeros = []
-    for k in range(lo):
-        zeros += [T["wa%d" % k][:, 256 * i:256 * i + 256] for i in range(max(k, 1))]
-    zeros += [T.wb[:, 256 * (7 - v):256 * (8 - v)] for v in range(0 if lo == 0 else 1, r + 1)]
-    S.wait_ge(sem.zz, 1)
-    for z in zeros:
-        S.activation(z, T.zb[:], COPY).then_inc(sem.sz, 1)
-    V.wait_ge(sem.zz, 1)
+    need(S, "s", zz)
+    for k, b in enumerate(chain):
+        w = PAD + 256 * SIZE[b]
+        S.activation(T["w%d" % k][:, 0:w], T.zb[:, 0:w], COPY).then_inc(sem["sz%d" % k], 1)
 
-    Y.wait_ge(sem.cv, 1)
-    Y.dma_start(T.litd[r], lb).then_inc(sem.st, 16)
-    Y.wait_ge(sem.sz, len(zeros))
-    nw = 0
+    need(Y, "y", cv)
+    Y.dma_start(T.litd[r], T.lb[:]).then_inc(sem.st, 16)
+    Y.wait_ge(sem.st, 16)
+    place = {}
+    for k, b in enumerate(chain):
+        for i in range(SIZE[b]):
+            place[b - i] = (k, PAD + 256 * i)
     for v in [r] + list(range(r)):
-        if v == r:
-            Y.wait_ge(sem.st, 16)
-        else:
-            Y.wait_ge(sem["lit%d" % v], got((v, fast if (v == 0 and r in fast) else lit_to[v])))
-        if v >= lo:
-            Y.dma_start(T.wb[0:128:16, 256 * (7 - v):256 * (8 - v)], T.litd[v]).then_inc(sem.dw, 16)
-            nw += 1
-        else:
-            Y.dma_start(T["wa%d" % v][0:128:16, 0:256], T.litd[v]).then_inc(sem["dz%d" % v], 16)
+        k, at = place[v]
+        need(Y, "y", "sz%d" % k)
+        if v != r:
+            Y.wait_ge(sem["lit%d" % v], got(v, fast if (v == 0 and r in fast) else lit_to[v]))
+        Y.dma_start(T["w%d" % k][0:128:16, at:at + 256], T.litd[v]).then_inc(sem["dw%d" % k], 16)
 
-    for k in range(lo):
-        nxt = T.wb if k == lo - 1 else T["wa%d" % (k + 1)]
-        at = BASE if k == lo - 1 else 256 * (k + 1)
-        S.wait_ge(sem["list%d" % k], got((k, list_to[k])))
-        S.wait_ge(sem["dz%d" % k], 16)
-        if k > 0:
-            S.wait_ge(sem.fw, k)
-        S.activation(nxt[:, at:at + 2048], T["wa%d" % k][:].indirect(T["land%d" % k][:, 0:128]), COPY).then_inc(sem.fw, 1)
-
-    end = BASE + (2048 if lo > 0 else 256)
-    win = T.wb[:, 256 * (7 - r):end]
-    for q in (V, S):
-        q.wait_ge(sem.dw, 16 * nw)
-        if lo > 0:
-            q.wait_ge(sem.fw, lo)
-        q.wait_ge(sem.so, 1)
-    V.tensor_copy(T.yo[:, 0:1024], win.indirect(T.offs[:, 0:64])).then_inc(sem.sg, 1)
-    S.activation(T.yo[:, 1024:2048], win.indirect(T.offs[:, 64:128]), COPY).then_inc(sem.sa, 1)
-    Y.wait_ge(sem.sg, 1)
+    made = []
+    for k, b in enumerate(chain):
+        last = b == r
+        end = PAD + 256 * SIZE[b] + (2048 if k > 0 else 0)
+        win = T["w%d" % k][:, 0:end]
+        if last:
+            lst, ready, out, at = T.offs, (offs, 1), T.yo, 0
+        else:
+            lst, ready = T["land%d" % b], ("list%d" % b, got(b, list_to[b]))
+            out, at = T["w%d" % (k + 1)], PAD + 256 * SIZE[chain[k + 1]]
+        mid = 0 if (n == 2 and k == 0) else 1024
+        cond = [("dw%d" % k, 16 * SIZE[b])] + made + [ready]
+        made = []
+        if mid > 0:
+            vneed(*cond)
+            made.append(vop(V.tensor_copy(out[:, at:at + mid], win.indirect(lst[:, 0:mid // 16]))))
+        need(S, "s", *cond)
+        made.append(vop(S.activation(out[:, at + mid:at + 2048], win.indirect(lst[:, mid // 16:128]), COPY)))
+    need(Y, "y", made[0])
     Y.dma_start(T.y[:, 0:1024], T.yo[0:128:16, 0:1024]).then_inc(sem.dy, 16)
-    S.wait_ge(sem.sa, 1)
+    need(S, "s", made[1])
     S.dma_start(T.y[:, 1024:2048], T.yo[0:128:16, 1024:2048]).then_inc(sem.dy, 16)
     Y.wait_ge(sem.dy, 32)

@@ -2,27 +2,30 @@ from concourse.bass import DstId, RemoteDMATransfer
 from concourse.mybir import dt, AluOpType, AxisListType, ActivationFunctionType
 
 N = 8
-PAD = 32
 BIG = 1.5 * 2.0 ** 35
 B16 = 1.5 * 2.0 ** 27
 B8 = 1.5 * 2.0 ** 26
-SIZE = [1, 1, 1, 2, 1, 2, 1, 2]
+PAIRS = {"32": (3, 2, [2, 3]), "54": (5, 4, [0, 1]), "76": (7, 6, [2, 3])}
+RAW = [p for p in PAIRS if sorted(PAIRS[p][2]) == sorted(PAIRS[p][:2])]
+PARTNER = {PAIRS[p][i]: PAIRS[p][1 - i] for p in RAW for i in (0, 1)}
+CHAIN = [["0"], ["0", "1"], ["0", "1", "2"], ["0", "1", "32"], ["0", "1", "32", "4"], ["0", "1", "32", "54"],
+         ["0", "1", "32", "54", "6"], ["0", "1", "32", "54", "76"]]
+SLOTS = {str(v): [v] for v in range(N)}
+SLOTS.update({p: [PAIRS[p][0], PAIRS[p][1]] for p in PAIRS})
+UPPER = {PAIRS[p][0]: p for p in PAIRS}
+LOWER = {PAIRS[p][1]: p for p in PAIRS}
+DOWN = range(N - 1, -1, -1)
+LIST_TO = {str(b): [q for q in DOWN if q != b and str(b) in CHAIN[q]] for b in range(N)}
+DEPTH = max(len(c) for c in CHAIN)
+FAST = [q for q in DOWN if len(CHAIN[q]) == DEPTH]
+LIT_TO = {v: [q for q in DOWN if q > v and not (v == 0 and q in FAST)] for v in range(N)}
 
 
-def below(r):
-    out, b = [], r - SIZE[r]
-    while b >= 0:
-        out.append(b)
-        b -= SIZE[b]
-    return out[::-1]
+def users(p, half):
+    return [q for q in DOWN if p in CHAIN[q] and q != PAIRS[p][2][half]]
 
-
-USED = sorted({b for r in range(N) for b in below(r)})
-DEPTH = max(len(below(r)) for r in range(N)) + 1
 
 SCRATCH = {
-    "fi": ("sbuf", [128, 1], "int32"),
-    "li": ("sbuf", [128, 1], "int32"),
     "lt": ("sbuf", [128, 16], "int32"),
     "lb": ("sbuf", [128, 16], "bfloat16"),
     "kp": ("sbuf", [128, 1], "int32"),
@@ -31,60 +34,69 @@ SCRATCH = {
     "kq": ("sbuf", [128, 128], "bfloat16"),
     "mq": ("sbuf", [128, 128], "bfloat16"),
     "kc": ("sbuf", [128, 128], "bfloat16"),
+    "kx": ("sbuf", [128, 128], "float32"),
+    "zb": ("sbuf", [128, 256], "bfloat16"),
     "nf": ("sbuf", [128, 1], "float32"),
     "pf": ("sbuf", [128, 1], "float32"),
     "mf": ("sbuf", [128, 1], "float32"),
+    "ce": ("sbuf", [128, 1], "float32"),
     "cs": ("sbuf", [128, 1], "float16"),
     "ch": ("sbuf", [128, 1], "float16"),
-    "cg": ("sbuf", [128, 1], "float16"),
     "tri": ("sbuf", [128, 128], "float16"),
     "ident": ("sbuf", [128, 128], "float16"),
     "nsh": ("sbuf", [128, 128], "float16"),
-    "dif": ("sbuf", [128, 128], "float16"),
     "mask": ("sbuf", [128, 128], "float16"),
     "mqm": ("sbuf", [128, 128], "float16"),
     "oh": ("sbuf", [128, 16], "float16"),
     "xa": ("sbuf", [128, 128], "float16"),
-    "f1": ("sbuf", [128, 1], "float16"),
-    "f2": ("sbuf", [128, 1], "float16"),
-    "ln16": ("sbuf", [128, 1], "float16"),
-    "hi": ("sbuf", [128, 1], "float32"),
-    "lo": ("sbuf", [128, 1], "float32"),
-    "r16": ("sbuf", [128, 1], "float32"),
-    "fr": ("sbuf", [128, 1], "float32"),
-    "rd": ("sbuf", [128, 1], "float32"),
-    "dm": ("sbuf", [128, 1], "float32"),
-    "tsb": ("sbuf", [128, 32], "float16"),
-    "tabs": ("sbuf", [128, 32], "float32"),
-    "tland": ("sbuf", [128, 32], "float32"),
-    "v1h": ("sbuf", [128, 128], "float16"),
-    "v2h": ("sbuf", [128, 128], "float16"),
-    "v1l": ("sbuf", [128, 128], "float16"),
-    "v2l": ("sbuf", [128, 128], "float16"),
-    "bst": ("sbuf", [128, 128], "float16"),
-    "xf": ("sbuf", [128, 128], "float16"),
-    "tt": ("sbuf", [128, 2048], "float16"),
-    "rr": ("sbuf", [128, 128], "float32"),
-    "xo": ("sbuf", [128, 128], "float16"),
     "offs": ("sbuf", [128, 128], "uint16"),
-    "zb": ("sbuf", [128, PAD + 512], "bfloat16"),
     "yo": ("sbuf", [128, 2048], "float32"),
     "litd": ("dram", [8, 128, 16], "bfloat16"),
-    "pa": ("psum", [128, 512], "float32"),
-    "pb": ("psum", [128, 512], "float32"),
-    "pd": ("psum", [128, 512], "float32"),
     "pt": ("psum", [128, 512], "float32"),
-    "p0": ("psum", [128, 512], "float32"),
-    "p1": ("psum", [128, 512], "float32"),
+    "q0": ("psum", [128, 512], "float32"),
+    "q1": ("psum", [128, 512], "float32"),
 }
-for _b in USED:
-    SCRATCH["land%d" % _b] = ("sbuf", [128, 128], "uint16")
+for _t in ("own", "far"):
+    SCRATCH.update({
+        "raw" + _t: ("sbuf", [128, 2], "int32"),
+        "f1" + _t: ("sbuf", [128, 1], "float16"),
+        "f2" + _t: ("sbuf", [128, 1], "float16"),
+        "ln" + _t: ("sbuf", [128, 1], "float16"),
+        "hi" + _t: ("sbuf", [128, 1], "float32"),
+        "lo" + _t: ("sbuf", [128, 1], "float32"),
+        "rs" + _t: ("sbuf", [128, 1], "float32"),
+        "fr" + _t: ("sbuf", [128, 1], "float32"),
+        "rd" + _t: ("sbuf", [128, 1], "float32"),
+        "dm" + _t: ("sbuf", [128, 1], "float32"),
+        "tsb" + _t: ("sbuf", [128, 32], "float16"),
+        "tab" + _t: ("sbuf", [128, 32], "float32"),
+        "v1h" + _t: ("sbuf", [128, 128], "float16"),
+        "v2h" + _t: ("sbuf", [128, 128], "float16"),
+        "v1l" + _t: ("sbuf", [128, 128], "float16"),
+        "v2l" + _t: ("sbuf", [128, 128], "float16"),
+        "bst" + _t: ("sbuf", [128, 128], "float16"),
+        "x" + _t: ("sbuf", [128, 128], "float16"),
+        "ps" + _t: ("psum", [128, 512], "float32"),
+        "pl" + _t: ("psum", [128, 512], "float32"),
+    })
+LANDS = [b for b in LIST_TO if LIST_TO[b]]
+SHIP = [p for p in PAIRS if p not in RAW]
+for _b in LANDS + list(PAIRS):
+    SCRATCH["land" + _b] = ("sbuf", [128, 128], "uint16")
+for _p in SHIP:
+    SCRATCH["x" + _p] = ("sbuf", [128, 128], "float16")
+    SCRATCH["t" + _p] = ("sbuf", [128, 32], "float32")
+for _k in range(2):
+    SCRATCH["tt%d" % _k] = ("sbuf", [128, 1024], "float16")
+    SCRATCH["rr%d" % _k] = ("sbuf", [128, 64], "float32")
+    SCRATCH["xo%d" % _k] = ("sbuf", [128, 64], "float16")
 for _k in range(DEPTH):
-    SCRATCH["w%d" % _k] = ("sbuf", [128, PAD + 256 if _k == 0 else PAD + 512 + 2048], "bfloat16")
-SEMAPHORES = (["di", "dl", "dlit", "st", "dy", "ls", "tabw"]
-              + ["a%d" % i for i in range(80)]
+    SCRATCH["w%d" % _k] = ("sbuf", [128, 256 if _k == 0 else 512 + 2048], "bfloat16")
+SEMAPHORES = (["di", "dl", "dlit", "st", "dy", "ls", "rawin"]
+              + ["a%d" % i for i in range(110)]
+              + ["xw" + p for p in SHIP] + ["tw" + p for p in SHIP] + ["half%s%d" % (p, h) for p in PAIRS for h in (0, 1)]
               + ["sz%d" % k for k in range(DEPTH)] + ["dw%d" % k for k in range(DEPTH)]
-              + ["lit%d" % v for v in range(N)] + ["list%d" % b for b in USED])
+              + ["lit%d" % v for v in range(N)] + ["list" + b for b in LANDS])
 
 
 def rank_program(g, core, T, topo):
@@ -95,9 +107,7 @@ def rank_program(g, core, T, topo):
     COPY = ActivationFunctionType.Copy
     sem = T.sem
     V, S, PE, Y = g.vector, g.scalar, g.tensor, g.sync
-    n = SIZE[r]
-    fwd = below(r)
-    chain = fwd + [r]
+    chain = CHAIN[r]
 
     def shared_engines(src, dsts):
         es = topo.engines(src, dsts[0])
@@ -124,12 +134,6 @@ def rank_program(g, core, T, topo):
     def got(v, ranks):
         return len(shared_engines(T.cores[v], [T.cores[d] for d in ranks]))
 
-    down = range(N - 1, -1, -1)
-    list_to = {b: [q for q in down if b in below(q)] for b in range(N)}
-    tab_to = {v: [q for q in range(N) if SIZE[q] == 2 and q == v + 1] for v in range(N)}
-    fast = [q for q in down if len(below(q)) == DEPTH - 1]
-    lit_to = {v: [q for q in down if q > v and not (v == 0 and q in fast)] for v in range(N)}
-
     count = [0]
     seen = set()
 
@@ -155,17 +159,22 @@ def rank_program(g, core, T, topo):
     def pneed(*ss):
         need(PE, "p", *ss)
 
-    S.dma_start(T.fi[:, 0:1], T.frm[:, :]).then_inc(sem.di, 16)
-    Y.dma_start(T.li[:, 0:1], T.ln[:, :]).then_inc(sem.dl, 16)
+    S.dma_start(T.rawown[:, 0:1], T.frm[:, :]).then_inc(sem.di, 16)
+    Y.dma_start(T.rawown[:, 1:2], T.ln[:, :]).then_inc(sem.dl, 16)
     S.dma_start(T.lt[:, :], T.lit[:, :]).then_inc(sem.dlit, 16)
 
     g0 = vop(g.iota(T.kp[:, 0:1], [[1, 1]], 0, 1))
     g1 = vop(g.iota(T.ki[:], [[1, 128]], 0, -1, allow_small_or_imprecise_dtypes=True))
     g2 = vop(g.iota(T.kq[:], [[16, 8], [0, 16]], 0, 0, allow_small_or_imprecise_dtypes=True))
     g3 = vop(g.iota(T.mq[:], [[0, 8], [1, 16]], 1, 0, allow_small_or_imprecise_dtypes=True))
+    if r in PARTNER:
+        need(g, "g", ("di", 16), ("dl", 16))
+        send([PARTNER[r]], T.rawown[:], T.rawfar[:], "rawin")
     g4 = vop(g.iota(T.kc[:], [[16, 128]], 0, 0, allow_small_or_imprecise_dtypes=True))
+    g5 = vop(g.iota(T.kx[:], [[16, 128]], 0, 1, allow_small_or_imprecise_dtypes=True))
+    zz = vop(g.iota(T.zb[:], [[0, 256]], 0, 0, allow_small_or_imprecise_dtypes=True))
 
-    zz = vop(V.memset(T.zb[:], 0.0))
+    tables = r in LOWER or (r in PARTNER and r in UPPER)
     vneed(g0)
     ka = vop(V.tensor_scalar(T.ka[:], T.kp[:], 15, None, A.bitwise_and))
     vneed(g1)
@@ -173,163 +182,233 @@ def rank_program(g, core, T, topo):
     ident = vop(V.tensor_scalar(T.ident[:], T.ki[:], 0, None, A.is_equal))
     vneed(ka)
     nf = vop(V.tensor_scalar(T.nf[:], T.ka[:], 15, -1, A.is_lt, A.mult))
+    ce = vop(V.tensor_scalar(T.ce[:], T.ka[:], 15, -2048, A.is_equal, A.mult))
     pf = vop(V.tensor_tensor(T.pf[:], T.kp[:], T.ka[:], A.subtract))
-    cs = vop(V.tensor_scalar(T.cs[:], T.ka[:], 0, -256 * n, A.mult, A.add))
     ch = vop(V.tensor_scalar(T.ch[:], T.ka[:], 0, -7.5, A.mult, A.add))
-    mf = vop(V.tensor_copy(T.mf[:], T.ka[:]))
+    if tables:
+        cs = vop(V.tensor_scalar(T.cs[:], T.ka[:], 0, -256, A.mult, A.add))
+        mf = vop(V.tensor_copy(T.mf[:], T.ka[:]))
     vneed(nf)
     nsh = vop(V.tensor_scalar(T.nsh[:], T.ki[:], 1, T.nf[:, 0:1], A.is_equal, A.mult))
-    vneed(pf)
-    cg = vop(V.tensor_scalar(T.cg[:], T.pf[:], -128, None, A.mult))
-    vneed(ident, nsh)
-    dif = vop(V.tensor_tensor(T.dif[:], T.ident[:], T.nsh[:], A.add))
-    vneed(g2)
+    vneed(pf, g2)
     mask = vop(V.tensor_scalar(T.mask[:], T.kq[:], T.pf[:, 0:1], None, A.is_equal))
+    place = []
+
+    def sums(t, v, wait_f, wait_l):
+        n = 2 if v in UPPER else 1
+        ps, raw = T["ps" + t], T["raw" + t]
+        s, k = new(), [0]
+
+        def mm(col, w, ws, x, xs, start, stop):
+            pneed(ws, xs)
+            PE.matmul(ps[:, col:col + 1], w[:], x[:], start, stop).then_inc(sem[s], 1)
+            k[0] += 1
+
+        vneed(wait_f)
+        f1 = vop(V.tensor_scalar(T["f1" + t][:], raw[:, 0:1], 2048, None, A.subtract))
+        f2 = vop(V.tensor_scalar(T["f2" + t][:], raw[:, 0:1], 2048, 2048 + 256 * n, A.is_lt, A.mult))
+        vneed(wait_l, ce)
+        l16 = vop(V.tensor_scalar(T["ln" + t][:], raw[:, 1:2], T.ce[:, 0:1], None, A.add))
+        low = v in LOWER
+        if low:
+            mm(2, T.ident, ident, T.cs, cs, True, False)
+            mm(2, T.nsh, nsh, T.cs, cs, False, False)
+        mm(2, T.ident, ident, T["f1" + t], f1, not low, False)
+        mm(2, T.nsh, nsh, T["f1" + t], f1, False, False)
+        mm(2, T.ident, ident, T["f2" + t], f2, False, False)
+        mm(2, T.nsh, nsh, T["f2" + t], f2, False, False)
+        mm(2, T.nsh, nsh, T["ln" + t], l16, False, True)
+        mm(1, T.ident, ident, T.ch, ch, True, False)
+        mm(1, T.tri, tri, T["ln" + t], l16, False, True)
+        mm(0, T.tri, tri, T["ln" + t], l16, True, True)
+        return s, k[0]
+
+    def table(t, s):
+        ps, tsb = T["ps" + t], T["tsb" + t]
+        vneed(s)
+        rd = vop(V.tensor_scalar(T["rd" + t][:], ps[:, 2:3], BIG, BIG, A.add, A.subtract))
+        vneed(oh)
+        t1 = vop(V.tensor_scalar(tsb[:, 0:16], T.oh[:], ps[:, 0:1], None, A.mult))
+        vneed(rd)
+        dm = vop(V.tensor_tensor(T["dm" + t][:], ps[:, 2:3], T["rd" + t][:], A.subtract))
+        vneed(dm)
+        t2 = vop(V.tensor_scalar(tsb[:, 16:32], T.oh[:], T["dm" + t][:, 0:1], None, A.mult))
+        pneed(mask, t1, t2)
+        pt = vop(PE.matmul(T.pt[:, 0:32], T.mask[:], tsb[:], True, True))
+        return pt
+
+    def table_out(t, pt):
+        vneed(pt)
+        return vop(V.tensor_copy(T["tab" + t][:], T.pt[:, 0:32]))
+
+    def codes(t, s, pt=None):
+        ps, tab = T["ps" + t], None
+        vneed(s)
+        hi = vop(V.tensor_scalar(T["hi" + t][:], ps[:, 2:3], B8, B8, A.add, A.subtract))
+        rs = vop(V.tensor_scalar(T["rs" + t][:], ps[:, 1:2], B16, B16, A.add, A.subtract))
+        vneed(hi)
+        lo = vop(V.tensor_tensor(T["lo" + t][:], ps[:, 2:3], T["hi" + t][:], A.subtract))
+        vneed(rs)
+        fr = vop(V.tensor_tensor(T["fr" + t][:], ps[:, 0:1], T["rs" + t][:], A.subtract))
+        if pt:
+            tab = table_out(t, pt)
+        vneed(g4)
+        a, b = T["rs" + t][:, 0:1], T["hi" + t][:, 0:1]
+        c = T["lo" + t][:, 0:1]
+        v1h = vop(V.tensor_scalar(T["v1h" + t][:], T.kc[:], a, b, A.is_gt, A.mult))
+        vneed(lo)
+        v1l = vop(V.tensor_scalar(T["v1l" + t][:], T.kc[:], a, c, A.is_gt, A.mult))
+        vneed(fr, mqm)
+        bst = vop(V.tensor_scalar(T["bst" + t][:], T.mqm[:], T["fr" + t][:, 0:1], None, A.is_gt))
+        v2h = vop(V.tensor_scalar(T["v2h" + t][:], T.kc[:], a, b, A.is_equal, A.mult))
+        v2l = vop(V.tensor_scalar(T["v2l" + t][:], T.kc[:], a, c, A.is_equal, A.mult))
+        if not place:
+            vneed(g5)
+            place.append(vop(V.tensor_scalar(T.xa[:], T.kx[:], T.pf[:, 0:1], None, A.subtract)))
+        z = new()
+        group = [(T.mask, mask, T["v1h" + t], v1h), (T.mask, mask, T["v1l" + t], v1l), (T["bst" + t], bst, T["v2h" + t], v2h),
+                 (T["bst" + t], bst, T["v2l" + t], v2l), (T.ident, ident, T.xa, place[0])]
+        for i, (w, ws, x, xs) in enumerate(group):
+            pneed(ws, xs)
+            PE.matmul(T["pl" + t][:, 0:128], w[:], x[:], i == 0, i == len(group) - 1).then_inc(sem[z], 1)
+        return (z, len(group)), tab
+
+    def literals():
+        V.wait_ge(sem.dlit, 16)
+        return vop(V.tensor_copy(T.lb[:], T.lt[:]))
+
+    def x_of(t, z):
+        vneed(z)
+        return vop(V.tensor_scalar(T["x" + t][:], T["pl" + t][:, 0:128], -512, None, A.add))
+
+    def offsets(z):
+        vneed(z)
+        return vop(V.tensor_scalar(T.offs[:], T.plown[:, 0:128], 256 if r in LOWER else 0, None, A.add))
+
+    so = sums("own", r, ("di", 16), ("dl", 16))
+    if r < 2:
+        cv = literals()
+    if tables:
+        vneed(mf, g3)
+        oh = vop(V.tensor_scalar(T.oh[:], T.mq[:, 0:16], 1, T.mf[:, 0:1], A.subtract, A.is_equal))
     vneed(g3, mask)
     mqm = vop(V.tensor_tensor(T.mqm[:], T.mq[:], T.mask[:], A.mult))
-    vneed(mf)
-    if tab_to[r]:
-        oh = vop(V.tensor_scalar(T.oh[:], T.mq[:, 0:16], 1, T.mf[:, 0:1], A.subtract, A.is_equal))
-
-    sd, sa, sb = new(), new(), new()
-    pneed(dif, cs, ident, cg, ch)
-    PE.matmul(T.pd[:, 0:1], T.dif[:], T.cs[:], True, False).then_inc(sem[sd], 1)
-    PE.matmul(T.pb[:, 0:1], T.ident[:], T.cg[:], True, False).then_inc(sem[sb], 1)
-    PE.matmul(T.pb[:, 0:1], T.ident[:], T.ch[:], False, False).then_inc(sem[sb], 1)
-    PE.matmul(T.pa[:, 0:1], T.ident[:], T.cg[:], True, False).then_inc(sem[sa], 1)
-
-    V.wait_ge(sem.di, 16)
-    f1 = vop(V.tensor_scalar(T.f1[:], T.fi[:], 2048, None, A.subtract))
-    f2 = vop(V.tensor_scalar(T.f2[:], T.fi[:], 2048, 2048 + 256 * n, A.is_lt, A.mult))
-    V.wait_ge(sem.dl, 16)
-    l16 = vop(V.tensor_copy(T.ln16[:], T.li[:]))
-    pneed(f1, f2)
-    PE.matmul(T.pd[:, 0:1], T.dif[:], T.f1[:], False, False).then_inc(sem[sd], 1)
-    PE.matmul(T.pd[:, 0:1], T.dif[:], T.f2[:], False, False).then_inc(sem[sd], 1)
-    pneed(l16, nsh, tri)
-    PE.matmul(T.pd[:, 0:1], T.nsh[:], T.ln16[:], False, True).then_inc(sem[sd], 1)
-    PE.matmul(T.pb[:, 0:1], T.tri[:], T.ln16[:], False, True).then_inc(sem[sb], 1)
-    PE.matmul(T.pa[:, 0:1], T.tri[:], T.ln16[:], False, True).then_inc(sem[sa], 1)
-    vneed(g4)
-    xa = vop(V.tensor_scalar(T.xa[:], T.kc[:], T.mf[:, 0:1], None, A.add))
-    V.wait_ge(sem.dlit, 16)
-    cv = vop(V.tensor_copy(T.lb[:], T.lt[:]))
-    sd, sa, sb = (sd, 4), (sa, 2), (sb, 3)
-    s0 = new()
-    pneed(xa)
-    PE.matmul(T.p0[:, 0:128], T.ident[:], T.xa[:], True, False).then_inc(sem[s0], 1)
-
-    vneed(sd)
-    if tab_to[r]:
-        rd = vop(V.tensor_scalar(T.rd[:], T.pd[:, 0:1], BIG, BIG, A.add, A.subtract))
-    hi = vop(V.tensor_scalar(T.hi[:], T.pd[:, 0:1], B8, B8, A.add, A.subtract))
-    vneed(sb)
-    r16 = vop(V.tensor_scalar(T.r16[:], T.pb[:, 0:1], B16, B16, A.add, A.subtract))
-    vneed(sa)
-    if tab_to[r]:
-        vneed(rd)
-        dm = vop(V.tensor_tensor(T.dm[:], T.pd[:, 0:1], T.rd[:], A.subtract))
-        vneed(oh)
-        t1 = vop(V.tensor_scalar(T.tsb[:, 0:16], T.oh[:], T.pa[:, 0:1], None, A.mult))
-        vneed(dm)
-        t2 = vop(V.tensor_scalar(T.tsb[:, 16:32], T.oh[:], T.dm[:, 0:1], None, A.mult))
-        pneed(mask, t1, t2)
-        pt = vop(PE.matmul(T.pt[:, 0:32], T.mask[:], T.tsb[:], True, True))
-    vneed(hi)
-    lo = vop(V.tensor_tensor(T.lo[:], T.pd[:, 0:1], T.hi[:], A.subtract))
-    vneed(r16)
-    fr = vop(V.tensor_tensor(T.fr[:], T.pa[:, 0:1], T.r16[:], A.subtract))
-    v1h = vop(V.tensor_scalar(T.v1h[:], T.kc[:], T.r16[:, 0:1], T.hi[:, 0:1], A.is_gt, A.mult))
-    if tab_to[r]:
-        vneed(pt)
-        tabs = vop(V.tensor_copy(T.tabs[:], T.pt[:, 0:32]))
-    v2h = vop(V.tensor_scalar(T.v2h[:], T.kc[:], T.r16[:, 0:1], T.hi[:, 0:1], A.is_equal, A.mult))
-    vneed(lo)
-    v1l = vop(V.tensor_scalar(T.v1l[:], T.kc[:], T.r16[:, 0:1], T.lo[:, 0:1], A.is_gt, A.mult))
-    vneed(fr, mqm)
-    bst = vop(V.tensor_scalar(T.bst[:], T.mqm[:], T.fr[:, 0:1], None, A.is_gt))
-    v2l = vop(V.tensor_scalar(T.v2l[:], T.kc[:], T.r16[:, 0:1], T.lo[:, 0:1], A.is_equal, A.mult))
-    pneed(mask, v1h)
-    PE.matmul(T.p0[:, 0:128], T.mask[:], T.v1h[:], False, False).then_inc(sem[s0], 1)
-    pneed(v1l)
-    PE.matmul(T.p0[:, 0:128], T.mask[:], T.v1l[:], False, False).then_inc(sem[s0], 1)
-    pneed(bst, v2h)
-    PE.matmul(T.p0[:, 0:128], T.bst[:], T.v2h[:], False, False).then_inc(sem[s0], 1)
-    pneed(v2l)
-    PE.matmul(T.p0[:, 0:128], T.bst[:], T.v2l[:], False, True).then_inc(sem[s0], 1)
-    vneed((s0, 5))
-    if n == 1:
-        offs = vop(V.tensor_scalar(T.offs[:], T.p0[:, 0:128], 256 * n + PAD, None, A.add))
+    xs, tabs = {}, {}
+    late = r in LOWER and r in PARTNER
+    pt = table("own", so) if r in LOWER else None
+    if late:
+        cv = literals()
+        tabs[r] = (T.tabown, table_out("own", pt))
     else:
-        xf = vop(V.tensor_copy(T.xf[:], T.p0[:, 0:128]))
+        z, tab = codes("own", so, pt)
+        if r in LOWER:
+            tabs[r] = (T.tabown, tab)
+        if r >= 2:
+            cv = literals()
+        if r in UPPER:
+            xs[r] = (T.xown, x_of("own", z))
+    if r in PARTNER:
+        far = PARTNER[r]
+        raw = ("rawin", got(far, [r]))
+        sf = sums("far", far, raw, raw)
+        if far in LOWER:
+            tabs[far] = (T.tabfar, table_out("far", table("far", sf)))
+        else:
+            xs[far] = (T.xfar, x_of("far", codes("far", sf)[0]))
+    if chain[-1] == str(r) and not late:
+        offs = offsets(z)
+
+    halves = [(p, h) for p in PAIRS for h in (0, 1) if PAIRS[p][2][h] == r]
+    done = {}
+    for i, (p, h) in enumerate(halves):
+        up, low, makers = PAIRS[p]
+        x, xw = xs[up] if up in xs else (T["x" + p], ("xw" + p, got(up, makers)))
+        tab, tw = tabs[low] if low in tabs else (T["t" + p], ("tw" + p, got(low, makers)))
+        x = x[:, 64 * h:64 * h + 64]
+        tt, rr, xo, ps = T["tt%d" % i], T["rr%d" % i], T["xo%d" % i], T["q%d" % i][:, 0:64]
         s1 = new()
-        vneed(xf)
-        V.wait_ge(sem.tabw, got(r - 1, tab_to[r - 1]))
-        pneed(xf)
-        PE.matmul(T.p1[:, 0:128], T.ident[:], T.xf[:], True, False).then_inc(sem[s1], 1)
+        vneed(xw, tw)
+        pneed(ident, xw)
+        PE.matmul(ps, T.ident[:], x, True, False).then_inc(sem[s1], 1)
         for k in range(16):
-            t = vop(V.tensor_scalar(T.tt[:, 128 * k:128 * k + 128], T.xf[:], T.tland[:, k:k + 1], T.tland[:, k + 16:k + 17],
-                                    A.is_ge, A.mult))
+            t = vop(V.tensor_scalar(tt[:, 64 * k:64 * k + 64], x, tab[:, k:k + 1], tab[:, k + 16:k + 17], A.is_ge, A.mult))
             pneed(t)
-            PE.matmul(T.p1[:, 0:128], T.ident[:], T.tt[:, 128 * k:128 * k + 128], False, k == 15).then_inc(sem[s1], 1)
+            PE.matmul(ps, T.ident[:], tt[:, 64 * k:64 * k + 64], False, k == 15).then_inc(sem[s1], 1)
         vneed((s1, 17))
-        rr = vop(V.tensor_scalar(T.rr[:], T.p1[:, 0:128], BIG, BIG, A.add, A.subtract))
-        vneed(rr)
-        xo = vop(V.tensor_tensor(T.xo[:], T.p1[:, 0:128], T.rr[:], A.subtract))
-        vneed(xo)
-        offs = vop(V.tensor_scalar(T.offs[:], T.xo[:], 256 * n + PAD, None, A.add))
+        a1 = vop(V.tensor_scalar(rr[:], ps, BIG, BIG, A.add, A.subtract))
+        vneed(a1)
+        a2 = vop(V.tensor_tensor(xo[:], ps, rr[:], A.subtract))
+        vneed(a2)
+        done[p, h] = vop(V.tensor_scalar(T["land" + p][:, 64 * h:64 * h + 64], xo[:], 512, None, A.add))
+    if late:
+        offs = offsets(codes("own", so)[0])
 
     if r == 0:
         need(g, "g", cv)
-        send(fast, T.lb[:], T.litd[0], "lit0")
-    if tab_to[r]:
-        need(g, "g", tabs)
-        send(tab_to[r], T.tabs[:], T.tland[:], "tabw")
-    if lit_to[r]:
+        send(FAST, T.lb[:], T.litd[0], "lit0")
+    if r in LOWER and LOWER[r] in SHIP:
+        need(g, "g", tabs[r][1])
+        send(PAIRS[LOWER[r]][2], T.tabown[:], T["t" + LOWER[r]][:], "tw" + LOWER[r])
+    if r in UPPER and UPPER[r] in SHIP:
+        need(g, "g", xs[r][1])
+        send(PAIRS[UPPER[r]][2], T.xown[:], T["x" + UPPER[r]][:], "xw" + UPPER[r])
+    if LIT_TO[r]:
         g.wait_ge(sem.st, 16)
-        send(lit_to[r], T.litd[r], T.litd[r], "lit%d" % r)
-    if list_to[r]:
+        send(LIT_TO[r], T.litd[r], T.litd[r], "lit%d" % r)
+    if LIST_TO[str(r)]:
         need(g, "g", offs)
-        send(list_to[r], T.offs[:], T["land%d" % r][:], "list%d" % r)
+        send(LIST_TO[str(r)], T.offs[:], T["land%d" % r][:], "list%d" % r)
+    for p, h in halves:
+        need(g, "g", done[p, h])
+        at = T["land" + p][:, 64 * h:64 * h + 64]
+        send(users(p, h), at, at, "half%s%d" % (p, h))
     if sent[0]:
         g.wait_ge(sem.ls, sent[0])
 
     need(S, "s", zz)
-    for k, b in enumerate(chain):
-        w = PAD + 256 * SIZE[b]
-        S.activation(T["w%d" % k][:, 0:w], T.zb[:, 0:w], COPY).then_inc(sem["sz%d" % k], 1)
+    for k in range(len(chain)):
+        for i in range(len(SLOTS[chain[k]])):
+            S.activation(T["w%d" % k][:, 256 * i:256 * i + 256], T.zb[:], COPY).then_inc(sem["sz%d" % k], 1)
 
     need(Y, "y", cv)
     Y.dma_start(T.litd[r], T.lb[:]).then_inc(sem.st, 16)
-    Y.wait_ge(sem.st, 16)
-    place = {}
+    spot = {}
     for k, b in enumerate(chain):
-        for i in range(SIZE[b]):
-            place[b - i] = (k, PAD + 256 * i)
-    for v in [r] + list(range(r)):
-        k, at = place[v]
-        need(Y, "y", "sz%d" % k)
-        if v != r:
-            Y.wait_ge(sem["lit%d" % v], got(v, fast if (v == 0 and r in fast) else lit_to[v]))
+        for i, v in enumerate(SLOTS[b]):
+            spot[v] = (k, 256 * i)
+    inw = [0] * len(chain)
+    for v in range(r + 1):
+        k, at = spot[v]
+        need(Y, "y", ("sz%d" % k, len(SLOTS[chain[k]])))
+        if v == r:
+            Y.wait_ge(sem.st, 16)
+        else:
+            Y.wait_ge(sem["lit%d" % v], got(v, FAST if (v == 0 and r in FAST) else LIT_TO[v]))
         Y.dma_start(T["w%d" % k][0:128:16, at:at + 256], T.litd[v]).then_inc(sem["dw%d" % k], 16)
+        inw[k] += 16
 
     made = []
     for k, b in enumerate(chain):
-        last = b == r
-        end = PAD + 256 * SIZE[b] + (2048 if k > 0 else 0)
+        end = 256 * len(SLOTS[b]) + (2048 if k > 0 else 0)
         win = T["w%d" % k][:, 0:end]
-        if last:
-            lst, ready, out, at = T.offs, (offs, 1), T.yo, 0
+        lst = T.offs if b == str(r) else T["land" + b]
+        if b == str(r):
+            ready = [offs, offs]
+        elif b in PAIRS:
+            ready = [done[b, h] if (b, h) in done else ("half%s%d" % (b, h), got(PAIRS[b][2][h], users(b, h))) for h in (0, 1)]
         else:
-            lst, ready = T["land%d" % b], ("list%d" % b, got(b, list_to[b]))
-            out, at = T["w%d" % (k + 1)], PAD + 256 * SIZE[chain[k + 1]]
-        mid = 0 if (n == 2 and k == 0) else 1024
-        cond = [("dw%d" % k, 16 * SIZE[b])] + made + [ready]
+            ready = [("list" + b, got(int(b), LIST_TO[b]))] * 2
+        if k == len(chain) - 1:
+            out, at = T.yo, 0
+        else:
+            out, at = T["w%d" % (k + 1)], 256 * len(SLOTS[chain[k + 1]])
+        cond = [("dw%d" % k, inw[k])] + made
         made = []
-        if mid > 0:
-            vneed(*cond)
+        mid = 0 if r in PARTNER and k == 0 else 1024
+        if mid:
+            vneed(*(cond + ready[:1]))
             made.append(vop(V.tensor_copy(out[:, at:at + mid], win.indirect(lst[:, 0:mid // 16]))))
-        need(S, "s", *cond)
+        need(S, "s", *(cond + ready[1:]))
         made.append(vop(S.activation(out[:, at + mid:at + 2048], win.indirect(lst[:, mid // 16:128]), COPY)))
     need(Y, "y", made[0])
     Y.dma_start(T.y[:, 0:1024], T.yo[0:128:16, 0:1024]).then_inc(sem.dy, 16)

from concourse.bass import DstId, RemoteDMATransfer
from concourse.mybir import dt, AluOpType, AxisListType, ActivationFunctionType

N = 8
BIG = 1.5 * 2.0 ** 35
B16 = 1.5 * 2.0 ** 27
B8 = 1.5 * 2.0 ** 26
PAIRS = {"32": (3, 2, [2, 3]), "54": (5, 4, [0, 1]), "76": (7, 6, [2, 3])}
RAW = [p for p in PAIRS if sorted(PAIRS[p][2]) == sorted(PAIRS[p][:2])]
PARTNER = {PAIRS[p][i]: PAIRS[p][1 - i] for p in RAW for i in (0, 1)}
CHAIN = [["0"], ["0", "1"], ["0", "1", "2"], ["0", "1", "32"], ["0", "1", "32", "4"], ["0", "1", "32", "54"],
         ["0", "1", "32", "54", "6"], ["0", "1", "32", "54", "76"]]
SLOTS = {str(v): [v] for v in range(N)}
SLOTS.update({p: [PAIRS[p][0], PAIRS[p][1]] for p in PAIRS})
UPPER = {PAIRS[p][0]: p for p in PAIRS}
LOWER = {PAIRS[p][1]: p for p in PAIRS}
DOWN = range(N - 1, -1, -1)
LIST_TO = {str(b): [q for q in DOWN if q != b and str(b) in CHAIN[q]] for b in range(N)}
DEPTH = max(len(c) for c in CHAIN)
FAST = [q for q in DOWN if len(CHAIN[q]) == DEPTH]
LIT_TO = {v: [q for q in DOWN if q > v and not (v == 0 and q in FAST)] for v in range(N)}


def users(p, half):
    return [q for q in DOWN if p in CHAIN[q] and q != PAIRS[p][2][half]]


SCRATCH = {
    "lt": ("sbuf", [128, 16], "int32"),
    "lb": ("sbuf", [128, 16], "bfloat16"),
    "kp": ("sbuf", [128, 1], "int32"),
    "ka": ("sbuf", [128, 1], "int32"),
    "ki": ("sbuf", [128, 128], "bfloat16"),
    "kq": ("sbuf", [128, 128], "bfloat16"),
    "mq": ("sbuf", [128, 128], "bfloat16"),
    "kc": ("sbuf", [128, 128], "bfloat16"),
    "kx": ("sbuf", [128, 128], "float32"),
    "zb": ("sbuf", [128, 256], "bfloat16"),
    "nf": ("sbuf", [128, 1], "float32"),
    "pf": ("sbuf", [128, 1], "float32"),
    "mf": ("sbuf", [128, 1], "float32"),
    "ce": ("sbuf", [128, 1], "float32"),
    "cs": ("sbuf", [128, 1], "float16"),
    "ch": ("sbuf", [128, 1], "float16"),
    "tri": ("sbuf", [128, 128], "float16"),
    "ident": ("sbuf", [128, 128], "float16"),
    "nsh": ("sbuf", [128, 128], "float16"),
    "mask": ("sbuf", [128, 128], "float16"),
    "mqm": ("sbuf", [128, 128], "float16"),
    "oh": ("sbuf", [128, 16], "float16"),
    "xa": ("sbuf", [128, 128], "float16"),
    "offs": ("sbuf", [128, 128], "uint16"),
    "yo": ("sbuf", [128, 2048], "float32"),
    "litd": ("dram", [8, 128, 16], "bfloat16"),
    "pt": ("psum", [128, 512], "float32"),
    "q0": ("psum", [128, 512], "float32"),
    "q1": ("psum", [128, 512], "float32"),
}
for _t in ("own", "far"):
    SCRATCH.update({
        "raw" + _t: ("sbuf", [128, 2], "int32"),
        "f1" + _t: ("sbuf", [128, 1], "float16"),
        "f2" + _t: ("sbuf", [128, 1], "float16"),
        "ln" + _t: ("sbuf", [128, 1], "float16"),
        "hi" + _t: ("sbuf", [128, 1], "float32"),
        "lo" + _t: ("sbuf", [128, 1], "float32"),
        "rs" + _t: ("sbuf", [128, 1], "float32"),
        "fr" + _t: ("sbuf", [128, 1], "float32"),
        "rd" + _t: ("sbuf", [128, 1], "float32"),
        "dm" + _t: ("sbuf", [128, 1], "float32"),
        "tsb" + _t: ("sbuf", [128, 32], "float16"),
        "tab" + _t: ("sbuf", [128, 32], "float32"),
        "v1h" + _t: ("sbuf", [128, 128], "float16"),
        "v2h" + _t: ("sbuf", [128, 128], "float16"),
        "v1l" + _t: ("sbuf", [128, 128], "float16"),
        "v2l" + _t: ("sbuf", [128, 128], "float16"),
        "bst" + _t: ("sbuf", [128, 128], "float16"),
        "x" + _t: ("sbuf", [128, 128], "float16"),
        "ps" + _t: ("psum", [128, 512], "float32"),
        "pl" + _t: ("psum", [128, 512], "float32"),
    })
LANDS = [b for b in LIST_TO if LIST_TO[b]]
SHIP = [p for p in PAIRS if p not in RAW]
for _b in LANDS + list(PAIRS):
    SCRATCH["land" + _b] = ("sbuf", [128, 128], "uint16")
for _p in SHIP:
    SCRATCH["x" + _p] = ("sbuf", [128, 128], "float16")
    SCRATCH["t" + _p] = ("sbuf", [128, 32], "float32")
for _k in range(2):
    SCRATCH["tt%d" % _k] = ("sbuf", [128, 1024], "float16")
    SCRATCH["rr%d" % _k] = ("sbuf", [128, 64], "float32")
    SCRATCH["xo%d" % _k] = ("sbuf", [128, 64], "float16")
for _k in range(DEPTH):
    SCRATCH["w%d" % _k] = ("sbuf", [128, 256 if _k == 0 else 512 + 2048], "bfloat16")
SEMAPHORES = (["di", "dl", "dlit", "st", "dy", "ls", "rawin"]
              + ["a%d" % i for i in range(110)]
              + ["xw" + p for p in SHIP] + ["tw" + p for p in SHIP] + ["half%s%d" % (p, h) for p in PAIRS for h in (0, 1)]
              + ["sz%d" % k for k in range(DEPTH)] + ["dw%d" % k for k in range(DEPTH)]
              + ["lit%d" % v for v in range(N)] + ["list" + b for b in LANDS])


def rank_program(g, core, T, topo):
    r = T.rank_of(core)
    if r is None:
        return
    A = AluOpType
    COPY = ActivationFunctionType.Copy
    sem = T.sem
    V, S, PE, Y = g.vector, g.scalar, g.tensor, g.sync
    chain = CHAIN[r]

    def shared_engines(src, dsts):
        es = topo.engines(src, dsts[0])
        for d in dsts[1:]:
            es = [e for e in es if e in topo.engines(src, d)]
        return es[:8]

    sent = [0]

    def send(ranks, src, dst, sname):
        cores = [T.cores[q] for q in ranks]
        es = shared_engines(core, cores)
        mask = 0
        for e in es:
            mask |= 1 << e
        ids = []
        for c in cores:
            rid, pid = topo.addr(c, core)
            ids.append(DstId(rid=rid, pnc=pid))
        g.remote_dma_fused([RemoteDMATransfer(dst_ids=ids, dma_engine_mask=mask, remote_sem=sem[sname], srcs=[src],
                                              dsts=[dst] * len(ids), alu_op=0)], local_sem=sem.ls)
        sent[0] += len(es)

    def got(v, ranks):
        return len(shared_engines(T.cores[v], [T.cores[d] for d in ranks]))

    count = [0]
    seen = set()

    def new():
        count[0] += 1
        return "a%d" % (count[0] - 1)

    def vop(ins):
        s = new()
        ins.then_inc(sem[s], 1)
        return s

    def need(q, name, *ss):
        for s in ss:
            s, k = s if isinstance(s, tuple) else (s, 1)
            if (name, s) not in seen:
                seen.add((name, s))
                q.wait_ge(sem[s], k)

    def vneed(*ss):
        need(V, "v", *ss)

    def pneed(*ss):
        need(PE, "p", *ss)

    S.dma_start(T.rawown[:, 0:1], T.frm[:, :]).then_inc(sem.di, 16)
    Y.dma_start(T.rawown[:, 1:2], T.ln[:, :]).then_inc(sem.dl, 16)
    S.dma_start(T.lt[:, :], T.lit[:, :]).then_inc(sem.dlit, 16)

    g0 = vop(g.iota(T.kp[:, 0:1], [[1, 1]], 0, 1))
    g1 = vop(g.iota(T.ki[:], [[1, 128]], 0, -1, allow_small_or_imprecise_dtypes=True))
    g2 = vop(g.iota(T.kq[:], [[16, 8], [0, 16]], 0, 0, allow_small_or_imprecise_dtypes=True))
    g3 = vop(g.iota(T.mq[:], [[0, 8], [1, 16]], 1, 0, allow_small_or_imprecise_dtypes=True))
    if r in PARTNER:
        need(g, "g", ("di", 16), ("dl", 16))
        send([PARTNER[r]], T.rawown[:], T.rawfar[:], "rawin")
    g4 = vop(g.iota(T.kc[:], [[16, 128]], 0, 0, allow_small_or_imprecise_dtypes=True))
    g5 = vop(g.iota(T.kx[:], [[16, 128]], 0, 1, allow_small_or_imprecise_dtypes=True))
    zz = vop(g.iota(T.zb[:], [[0, 256]], 0, 0, allow_small_or_imprecise_dtypes=True))

    tables = r in LOWER or (r in PARTNER and r in UPPER)
    vneed(g0)
    ka = vop(V.tensor_scalar(T.ka[:], T.kp[:], 15, None, A.bitwise_and))
    vneed(g1)
    tri = vop(V.tensor_scalar(T.tri[:], T.ki[:], 0, None, A.is_gt))
    ident = vop(V.tensor_scalar(T.ident[:], T.ki[:], 0, None, A.is_equal))
    vneed(ka)
    nf = vop(V.tensor_scalar(T.nf[:], T.ka[:], 15, -1, A.is_lt, A.mult))
    ce = vop(V.tensor_scalar(T.ce[:], T.ka[:], 15, -2048, A.is_equal, A.mult))
    pf = vop(V.tensor_tensor(T.pf[:], T.kp[:], T.ka[:], A.subtract))
    ch = vop(V.tensor_scalar(T.ch[:], T.ka[:], 0, -7.5, A.mult, A.add))
    if tables:
        cs = vop(V.tensor_scalar(T.cs[:], T.ka[:], 0, -256, A.mult, A.add))
        mf = vop(V.tensor_copy(T.mf[:], T.ka[:]))
    vneed(nf)
    nsh = vop(V.tensor_scalar(T.nsh[:], T.ki[:], 1, T.nf[:, 0:1], A.is_equal, A.mult))
    vneed(pf, g2)
    mask = vop(V.tensor_scalar(T.mask[:], T.kq[:], T.pf[:, 0:1], None, A.is_equal))
    place = []

    def sums(t, v, wait_f, wait_l):
        n = 2 if v in UPPER else 1
        ps, raw = T["ps" + t], T["raw" + t]
        s, k = new(), [0]

        def mm(col, w, ws, x, xs, start, stop):
            pneed(ws, xs)
            PE.matmul(ps[:, col:col + 1], w[:], x[:], start, stop).then_inc(sem[s], 1)
            k[0] += 1

        vneed(wait_f)
        f1 = vop(V.tensor_scalar(T["f1" + t][:], raw[:, 0:1], 2048, None, A.subtract))
        f2 = vop(V.tensor_scalar(T["f2" + t][:], raw[:, 0:1], 2048, 2048 + 256 * n, A.is_lt, A.mult))
        vneed(wait_l, ce)
        l16 = vop(V.tensor_scalar(T["ln" + t][:], raw[:, 1:2], T.ce[:, 0:1], None, A.add))
        low = v in LOWER
        if low:
            mm(2, T.ident, ident, T.cs, cs, True, False)
            mm(2, T.nsh, nsh, T.cs, cs, False, False)
        mm(2, T.ident, ident, T["f1" + t], f1, not low, False)
        mm(2, T.nsh, nsh, T["f1" + t], f1, False, False)
        mm(2, T.ident, ident, T["f2" + t], f2, False, False)
        mm(2, T.nsh, nsh, T["f2" + t], f2, False, False)
        mm(2, T.nsh, nsh, T["ln" + t], l16, False, True)
        mm(1, T.ident, ident, T.ch, ch, True, False)
        mm(1, T.tri, tri, T["ln" + t], l16, False, True)
        mm(0, T.tri, tri, T["ln" + t], l16, True, True)
        return s, k[0]

    def table(t, s):
        ps, tsb = T["ps" + t], T["tsb" + t]
        vneed(s)
        rd = vop(V.tensor_scalar(T["rd" + t][:], ps[:, 2:3], BIG, BIG, A.add, A.subtract))
        vneed(oh)
        t1 = vop(V.tensor_scalar(tsb[:, 0:16], T.oh[:], ps[:, 0:1], None, A.mult))
        vneed(rd)
        dm = vop(V.tensor_tensor(T["dm" + t][:], ps[:, 2:3], T["rd" + t][:], A.subtract))
        vneed(dm)
        t2 = vop(V.tensor_scalar(tsb[:, 16:32], T.oh[:], T["dm" + t][:, 0:1], None, A.mult))
        pneed(mask, t1, t2)
        pt = vop(PE.matmul(T.pt[:, 0:32], T.mask[:], tsb[:], True, True))
        return pt

    def table_out(t, pt):
        vneed(pt)
        return vop(V.tensor_copy(T["tab" + t][:], T.pt[:, 0:32]))

    def codes(t, s, pt=None):
        ps, tab = T["ps" + t], None
        vneed(s)
        hi = vop(V.tensor_scalar(T["hi" + t][:], ps[:, 2:3], B8, B8, A.add, A.subtract))
        rs = vop(V.tensor_scalar(T["rs" + t][:], ps[:, 1:2], B16, B16, A.add, A.subtract))
        vneed(hi)
        lo = vop(V.tensor_tensor(T["lo" + t][:], ps[:, 2:3], T["hi" + t][:], A.subtract))
        vneed(rs)
        fr = vop(V.tensor_tensor(T["fr" + t][:], ps[:, 0:1], T["rs" + t][:], A.subtract))
        if pt:
            tab = table_out(t, pt)
        vneed(g4)
        a, b = T["rs" + t][:, 0:1], T["hi" + t][:, 0:1]
        c = T["lo" + t][:, 0:1]
        v1h = vop(V.tensor_scalar(T["v1h" + t][:], T.kc[:], a, b, A.is_gt, A.mult))
        vneed(lo)
        v1l = vop(V.tensor_scalar(T["v1l" + t][:], T.kc[:], a, c, A.is_gt, A.mult))
        vneed(fr, mqm)
        bst = vop(V.tensor_scalar(T["bst" + t][:], T.mqm[:], T["fr" + t][:, 0:1], None, A.is_gt))
        v2h = vop(V.tensor_scalar(T["v2h" + t][:], T.kc[:], a, b, A.is_equal, A.mult))
        v2l = vop(V.tensor_scalar(T["v2l" + t][:], T.kc[:], a, c, A.is_equal, A.mult))
        if not place:
            vneed(g5)
            place.append(vop(V.tensor_scalar(T.xa[:], T.kx[:], T.pf[:, 0:1], None, A.subtract)))
        z = new()
        group = [(T.mask, mask, T["v1h" + t], v1h), (T.mask, mask, T["v1l" + t], v1l), (T["bst" + t], bst, T["v2h" + t], v2h),
                 (T["bst" + t], bst, T["v2l" + t], v2l), (T.ident, ident, T.xa, place[0])]
        for i, (w, ws, x, xs) in enumerate(group):
            pneed(ws, xs)
            PE.matmul(T["pl" + t][:, 0:128], w[:], x[:], i == 0, i == len(group) - 1).then_inc(sem[z], 1)
        return (z, len(group)), tab

    def literals():
        V.wait_ge(sem.dlit, 16)
        return vop(V.tensor_copy(T.lb[:], T.lt[:]))

    def x_of(t, z):
        vneed(z)
        return vop(V.tensor_scalar(T["x" + t][:], T["pl" + t][:, 0:128], -512, None, A.add))

    def offsets(z):
        vneed(z)
        return vop(V.tensor_scalar(T.offs[:], T.plown[:, 0:128], 256 if r in LOWER else 0, None, A.add))

    so = sums("own", r, ("di", 16), ("dl", 16))
    if r < 2:
        cv = literals()
    if tables:
        vneed(mf, g3)
        oh = vop(V.tensor_scalar(T.oh[:], T.mq[:, 0:16], 1, T.mf[:, 0:1], A.subtract, A.is_equal))
    vneed(g3, mask)
    mqm = vop(V.tensor_tensor(T.mqm[:], T.mq[:], T.mask[:], A.mult))
    xs, tabs = {}, {}
    late = r in LOWER and r in PARTNER
    pt = table("own", so) if r in LOWER else None
    if late:
        cv = literals()
        tabs[r] = (T.tabown, table_out("own", pt))
    else:
        z, tab = codes("own", so, pt)
        if r in LOWER:
            tabs[r] = (T.tabown, tab)
        if r >= 2:
            cv = literals()
        if r in UPPER:
            xs[r] = (T.xown, x_of("own", z))
    if r in PARTNER:
        far = PARTNER[r]
        raw = ("rawin", got(far, [r]))
        sf = sums("far", far, raw, raw)
        if far in LOWER:
            tabs[far] = (T.tabfar, table_out("far", table("far", sf)))
        else:
            xs[far] = (T.xfar, x_of("far", codes("far", sf)[0]))
    if chain[-1] == str(r) and not late:
        offs = offsets(z)

    halves = [(p, h) for p in PAIRS for h in (0, 1) if PAIRS[p][2][h] == r]
    done = {}
    for i, (p, h) in enumerate(halves):
        up, low, makers = PAIRS[p]
        x, xw = xs[up] if up in xs else (T["x" + p], ("xw" + p, got(up, makers)))
        tab, tw = tabs[low] if low in tabs else (T["t" + p], ("tw" + p, got(low, makers)))
        x = x[:, 64 * h:64 * h + 64]
        tt, rr, xo, ps = T["tt%d" % i], T["rr%d" % i], T["xo%d" % i], T["q%d" % i][:, 0:64]
        s1 = new()
        vneed(xw, tw)
        pneed(ident, xw)
        PE.matmul(ps, T.ident[:], x, True, False).then_inc(sem[s1], 1)
        for k in range(16):
            t = vop(V.tensor_scalar(tt[:, 64 * k:64 * k + 64], x, tab[:, k:k + 1], tab[:, k + 16:k + 17], A.is_ge, A.mult))
            pneed(t)
            PE.matmul(ps, T.ident[:], tt[:, 64 * k:64 * k + 64], False, k == 15).then_inc(sem[s1], 1)
        vneed((s1, 17))
        a1 = vop(V.tensor_scalar(rr[:], ps, BIG, BIG, A.add, A.subtract))
        vneed(a1)
        a2 = vop(V.tensor_tensor(xo[:], ps, rr[:], A.subtract))
        vneed(a2)
        done[p, h] = vop(V.tensor_scalar(T["land" + p][:, 64 * h:64 * h + 64], xo[:], 512, None, A.add))
    if late:
        offs = offsets(codes("own", so)[0])

    if r == 0:
        need(g, "g", cv)
        send(FAST, T.lb[:], T.litd[0], "lit0")
    if r in LOWER and LOWER[r] in SHIP:
        need(g, "g", tabs[r][1])
        send(PAIRS[LOWER[r]][2], T.tabown[:], T["t" + LOWER[r]][:], "tw" + LOWER[r])
    if r in UPPER and UPPER[r] in SHIP:
        need(g, "g", xs[r][1])
        send(PAIRS[UPPER[r]][2], T.xown[:], T["x" + UPPER[r]][:], "xw" + UPPER[r])
    if LIT_TO[r]:
        g.wait_ge(sem.st, 16)
        send(LIT_TO[r], T.litd[r], T.litd[r], "lit%d" % r)
    if LIST_TO[str(r)]:
        need(g, "g", offs)
        send(LIST_TO[str(r)], T.offs[:], T["land%d" % r][:], "list%d" % r)
    for p, h in halves:
        need(g, "g", done[p, h])
        at = T["land" + p][:, 64 * h:64 * h + 64]
        send(users(p, h), at, at, "half%s%d" % (p, h))
    if sent[0]:
        g.wait_ge(sem.ls, sent[0])

    need(S, "s", zz)
    for k in range(len(chain)):
        for i in range(len(SLOTS[chain[k]])):
            S.activation(T["w%d" % k][:, 256 * i:256 * i + 256], T.zb[:], COPY).then_inc(sem["sz%d" % k], 1)

    need(Y, "y", cv)
    Y.dma_start(T.litd[r], T.lb[:]).then_inc(sem.st, 16)
    spot = {}
    for k, b in enumerate(chain):
        for i, v in enumerate(SLOTS[b]):
            spot[v] = (k, 256 * i)
    inw = [0] * len(chain)
    for v in range(r + 1):
        k, at = spot[v]
        need(Y, "y", ("sz%d" % k, len(SLOTS[chain[k]])))
        if v == r:
            Y.wait_ge(sem.st, 16)
        else:
            Y.wait_ge(sem["lit%d" % v], got(v, FAST if (v == 0 and r in FAST) else LIT_TO[v]))
        Y.dma_start(T["w%d" % k][0:128:16, at:at + 256], T.litd[v]).then_inc(sem["dw%d" % k], 16)
        inw[k] += 16

    made = []
    for k, b in enumerate(chain):
        end = 256 * len(SLOTS[b]) + (2048 if k > 0 else 0)
        win = T["w%d" % k][:, 0:end]
        lst = T.offs if b == str(r) else T["land" + b]
        if b == str(r):
            ready = [offs, offs]
        elif b in PAIRS:
            ready = [done[b, h] if (b, h) in done else ("half%s%d" % (b, h), got(PAIRS[b][2][h], users(b, h))) for h in (0, 1)]
        else:
            ready = [("list" + b, got(int(b), LIST_TO[b]))] * 2
        if k == len(chain) - 1:
            out, at = T.yo, 0
        else:
            out, at = T["w%d" % (k + 1)], 256 * len(SLOTS[chain[k + 1]])
        cond = [("dw%d" % k, inw[k])] + made
        made = []
        mid = 0 if r in PARTNER and k == 0 else 1024
        if mid:
            vneed(*(cond + ready[:1]))
            made.append(vop(V.tensor_copy(out[:, at:at + mid], win.indirect(lst[:, 0:mid // 16]))))
        need(S, "s", *(cond + ready[1:]))
        made.append(vop(S.activation(out[:, at + mid:at + 2048], win.indirect(lst[:, mid // 16:128]), COPY)))
    need(Y, "y", made[0])
    Y.dma_start(T.y[:, 0:1024], T.yo[0:128:16, 0:1024]).then_inc(sem.dy, 16)
    need(S, "s", made[1])
    S.dma_start(T.y[:, 1024:2048], T.yo[0:128:16, 1024:2048]).then_inc(sem.dy, 16)
    Y.wait_ge(sem.dy, 32)
